import numpy as np, ml_dtypes
CORES = [36,164,52,180,100,228,116,244]
N = 8
import mx_ref
BF = ml_dtypes.bfloat16
def gentries(a):
    return np.ascontiguousarray(a.reshape(8, 16, -1).transpose(0, 2, 1)).reshape(8, -1)
def gtable(e):
    e = np.asarray(e); return np.ascontiguousarray(e.reshape(8, -1, 16).transpose(0, 2, 1)).reshape(128, -1).astype(np.int32)
def gcols(t, e):
    v = np.concatenate([t.reshape(8, 16, -1, 4), np.zeros((8, 16, 1, 4), BF)], axis=2)
    return np.ascontiguousarray(np.stack([v[g][:, e[g]] for g in range(8)])).reshape(128, -1)
def tile(rs):
    return np.stack(rs, axis=2).reshape(128, -1).astype(BF)
def pick(q, e):
    c = np.concatenate([q[0].reshape(128, -1, 4), np.zeros((128, 1, 4), np.uint8)], axis=1); s = np.concatenate([q[1], np.ones((16, 1), np.uint8)], axis=1)
    return (np.ascontiguousarray(c[:, e].reshape(128, -1)), np.ascontiguousarray(s[:, e]))
def join(*qs):
    return (np.concatenate([q[0] for q in qs], axis=1), np.concatenate([q[1] for q in qs], axis=1))
def put(q, e, v):
    c, s = q[0].reshape(128, -1, 4).copy(), q[1].copy(); c[:, e] = v[0].reshape(128, -1, 4); s[:, e] = v[1]
    return (c.reshape(128, -1), s)
def pk(c, s):
    return (np.ascontiguousarray(c), mx_ref.live(s))
def emit(q):
    return q[0], q[1]
def packed(v, rng):
    q = [mx_ref.quantize(np.ascontiguousarray(v[r])) for r in range(N)]
    return np.stack([a for a, b in q]), np.stack([mx_ref.plane(b, rng) for a, b in q])
def values_of_codes():
    e, c = np.zeros((128, 128, 4), np.float32), np.zeros((128, 2, 4), np.uint8)
    e[np.arange(128), np.arange(128), 0] = 1
    c[:127, :, 0] = np.arange(256).reshape(2, 128).T[:127]
    return mx_ref.matmul(mx_ref.quantize(e.reshape(128, 512).astype(BF)), (c.reshape(128, 8), np.full((16, 2), 127, np.uint8))).T.reshape(-1).astype(np.float64)
CODE_VALUE, SCALE_VALUE = values_of_codes(), 2.0 ** (np.arange(256) - 127.0)
def decode(q):
    return (CODE_VALUE[q[0]].reshape(16, 8, -1, 4) * SCALE_VALUE[q[1]][:, None, :, None] + 0.0).reshape(128, -1).astype(np.float32)
def f(rng, *shape):
    return mx_ref.flush((rng.standard_normal(shape, dtype=np.float32) * np.exp2(rng.integers(-2, 3, shape[:-1] + (1,)))).astype(BF))
def wide(rng, *shape, cols=0):
    v = rng.standard_normal(shape, dtype=np.float32) * np.exp2(rng.integers(-12, 13, shape)).astype(np.float32)
    if cols: v *= np.repeat(np.exp2(rng.integers(-cols, cols + 1, shape[:-2] + (1, shape[-1] // 4))) * (rng.random(shape[:-2] + (1, shape[-1] // 4)) > 0.0625), 4, axis=-1).astype(np.float32)
    return mx_ref.flush(v.astype(BF))
C, L, S, R = 288, 48, 12, 3
G = np.arange(8)[:, None]
def big(v):
    v = v.astype(np.float32)
    v[np.abs(v) < np.float32(2.0 ** -16)] = 0
    return v.astype(BF)
def numbers_of(rng):
    u = np.array(f(rng, N, 128, 512)).reshape(N, 8, 16, 128, 4)
    for g in range(8):
        u[:, :g, :, 16 * g] = 0
        u[:, g + 1:, :, 16 * g] = 0
    return {"x": big(f(rng, N, 128, 4 * C)), "u": u.reshape(N, 128, 512), "v": np.array(f(rng, N, 128, 512))}
def layers(rng):
    return big(f(rng, N, 128, 2048)).reshape(N, 8, 16, 4, 8, 16, 4)
def weights(rng, w):
    c, p = packed(np.ascontiguousarray(w).reshape(N, 128, 2048), rng)
    return {"wc": c, "ws": p}
def routes(rng):
    return np.argsort(rng.random((N, 8, 2 * C)), axis=2) % C
def walks(rng):
    return rng.integers(0, C, (N, 8, C))
def ways(e, w):
    return {"rt": np.stack([gtable(a) for a in e]), "ft": np.stack([gtable(a) for a in w])}
def setup_inputs(rng):
    return {**numbers_of(rng), **weights(rng, layers(rng)), **ways(routes(rng), walks(rng))}
def setup_inputs_ties(rng):
    d = numbers_of(rng)
    e = rng.permutation(N)
    x = d["x"].reshape(N, 8, 16, C, 4)
    a = x[0][:, :8, :3].copy()
    a[:, :, 2] = 0
    for r in range(N):
        k = rng.permutation(C) % 3
        if r == e[0]: k = np.zeros(C, int)
        if r == e[1]: k = np.full(C, 2)
        x[r][:, :8] = a[:, :, k]
    u = d["u"].reshape(N, 8, 16, 128, 4)
    u[:, :, 8:, ::16] = 0
    w = layers(rng)
    w[:, :, :, :, :, :8] = 0
    return {"x": x.reshape(N, 128, 4 * C), "u": u.reshape(N, 128, 512), "v": d["v"], **weights(rng, w), **ways(routes(rng), walks(rng))}
def setup_inputs_near(rng):
    d = numbers_of(rng)
    x = np.zeros((N, 8, 16, C, 4), np.float32)
    u = d["u"].reshape(N, 128, 128, 4)
    u[:, :, ::16] = 0
    o, c = rng.permutation(N) % 4, rng.permutation(8) % 2 * 2.0 - 1.0
    e = np.zeros((N, 8, 2 * C), int)
    for r in range(N):
        i = (np.arange(C) + rng.integers(0, C, (8, 1))) % C
        e[r, :, :C] = np.argsort(i, axis=1)
        e[r, :, C:] = np.argsort(rng.random((8, C)), axis=1)
        size = 1.0 if o[r] < 2 else 2.0 ** -4
        z = (((i // 2)[:, :, None] >> np.arange(8)) & 1) * np.exp2(np.arange(8) - 23.0) * size
        x[r, :, 0, :, 0] = c[:, None] * (1 - r % 2 * 2) if o[r] < 2 else (8 + i % 2) * 2.0 ** -30
        x[r, :, 8] = z[:, :, :4]
        x[r, :, 9] = z[:, :, 4:]
        x[r, :, 10:] = rng.integers(4, 8, (8, 6, C, 4)) * 2.0 ** -20 * size
        k = 1.0 if o[r] == 0 else 2.0 ** -30
        for h in range(0, 128, 16):
            u[r, h, h, 0] = k
            u[r, h + 8:h + 10, h] = k
    w = layers(rng)
    w[:, :, :10] = 0
    w[:, :, :, :, :, :10] = 0
    return {"x": x.reshape(N, 128, 4 * C).astype(BF), "u": u.reshape(N, 128, 512), "v": d["v"], **weights(rng, w), **ways(e, walks(rng))}
def setup_inputs_huge(rng):
    d = numbers_of(rng)
    c = np.stack([np.where(rng.permutation(C) % 2 == 0, -1.0, 0.25) for r in range(N)])
    c[rng.permutation(N) < N // 2] = -1
    x = 2.0 ** 30 * (0.8 + 0.2 * rng.random((N, 128, C, 4))) * c[:, None, :, None]
    s = np.stack([rng.permutation(8) % 2 * 2.0 - 1.0 for r in range(N)])
    a = 2.0 ** 30 * (1 - 0.1 * rng.random((N, 8, 16, 4))) * s[:, :, None, None]
    u = d["u"].reshape(N, 8, 16, 128, 4)
    for g in range(8): u[:, g, :, 16 * g] = a[:, g].astype(np.float32).astype(BF)
    w = np.zeros((N, 128, 4, 128, 4), np.float32)
    i = np.arange(128)
    for b in range(4): w[:, i, b, i, b] = -4
    return {"x": x.astype(np.float32).reshape(N, 128, 4 * C).astype(BF), "u": u.reshape(N, 128, 512), "v": d["v"], **weights(rng, w.astype(BF)), **ways(routes(rng), walks(rng))}
def setup_inputs_routes(rng):
    d = numbers_of(rng)
    x, u = d["x"].reshape(N, 8, 16, C, 4), d["u"].astype(np.float32).reshape(N, 8, 16, 128, 4)
    e, w = routes(rng), walks(rng)
    n = np.arange(C)
    for r in range(N):
        for g, k in enumerate(rng.permutation(8)):
            p = rng.permutation(C)
            if k == 0: e[r, g], w[r, g] = np.concatenate([p, p]), n
            if k == 1: e[r, g], w[r, g] = np.repeat(p, 2), (n + 1) % C
            if k == 2: e[r, g], w[r, g] = np.concatenate([p, p[::-1]]), (n - 1) % C
            if k == 3: e[r, g], w[r, g] = np.tile(p.reshape(L, S // 2), 2).reshape(-1), p[0]
            if k == 4:
                a = np.zeros((L, S), int)
                a[:, 0] = np.tile(p[:L // 2], 2)
                a[:, 1:] = rng.permutation(np.tile(p[L // 2:], 2)).reshape(L, S - 1)
                e[r, g], w[r, g] = a.reshape(-1), n ^ 1
            if k == 5:
                w[r, g] = e[r, g, 1]
                x[r, g, :, e[r, g, 0]] = (16 * np.sign(u[r, g, :, 16 * g])).astype(BF)
    return {"x": x.reshape(N, 128, 4 * C), "u": d["u"], "v": d["v"], **weights(rng, layers(rng)), **ways(e, w)}
def setup_inputs_spread(rng):
    d = setup_inputs(rng)
    d["x"] = big(wide(rng, N, 128, 4 * C, cols=6))
    return d
def check_inputs(d):
    b = []
    for k in ("x", "u", "v"):
        a = np.abs(d[k].astype(np.float32))
        if not (np.isfinite(a).all() and ((a == 0) | (a >= 2.0 ** -30) & (a <= 2.0 ** 30)).all()): b.append("a value of " + k)
    a = d["u"].astype(np.float32).reshape(N, 8, 16, 128, 4)
    for g in range(8):
        if (np.delete(a[:, :, :, 16 * g], g, axis=1) != 0).any(): b.append("u: a column that scores a group isn't zero outside it")
    none, least, most = [emit(mx_ref.quantize(np.full((128, 16), k, np.float32).astype(BF)))[1][0, 0] for k in (0.0, 2.0 ** -30, 2.0 ** 30)]
    for r in range(N):
        if ((d["wc"][r] == 0x7F) | (d["wc"][r] == 0xFF)).any(): b.append("wc: a code that is no number")
        s = mx_ref.live(d["ws"][r])
        if ((s != none) & ((s < least) | (s > most))).any(): b.append("ws: a scale out of range")
        if (np.sort(gentries(d["rt"][r]), axis=1) != np.arange(2 * C) // 2).any(): b.append("rt: a stop that isn't there exactly twice")
    if ((d["ft"] < 0) | (d["ft"] >= C)).any(): b.append("ft: a number that is no stop")
    return b
def reference(x, u, v, wc, ws, rt, ft):
    qu = [mx_ref.quantize(u[r]) for r in range(N)]
    lay = [pk(wc[r], ws[r]) for r in range(N)]
    way = [gentries(rt[r]) for r in range(N)]
    foot = [gentries(ft[r]) for r in range(N)]
    at = [np.argsort(way[r], axis=1, kind="stable").reshape(8, C, 2) for r in range(N)]
    now = [x[r] for r in range(N)]
    last = [None] * N
    for t in range(R):
        own, score, sent = [], [], []
        for r in range(N):
            q = mx_ref.quantize(now[r])
            s = mx_ref.matmul(qu[r], q)[::16] + np.float32(0.0)
            z = s[G, way[r]].reshape(8, L, S)
            e = np.take_along_axis(way[r].reshape(8, L, S), np.argmax(z, axis=2)[:, :, None], axis=2)[:, :, 0]
            own.append(decode(q))
            score.append(z)
            sent.append(mx_ref.quantize(gcols(now[r], e)))
        for r in range(N):
            guests = sent[(r - 1 - t) % N]
            z = mx_ref.matmul(qu[r], guests)[::16] + np.float32(0.0)
            c = np.concatenate([z[:, :, None], score[r][:, :, :S - 1]], axis=2)
            src = np.concatenate([np.tile(C + np.arange(L), (8, 1))[:, :, None], way[r].reshape(8, L, S)[:, :, :S - 1]], axis=2)
            m = np.maximum.accumulate(c, axis=2)
            above = np.zeros((8, L, S), bool)
            above[:, :, 1:] = c[:, :, 1:] > m[:, :, :-1]
            k = np.maximum.accumulate(np.where(above, np.arange(S), 0), axis=2)
            a, val = np.take_along_axis(src, k, axis=2).reshape(8, -1), m.reshape(8, -1)
            p0, p1 = at[r][:, :, 0], at[r][:, :, 1]
            p = np.where(val[G, p1] > val[G, p0], p1, p0)
            a, val = a[G, p], val[G, p]
            a = a[G, np.where(val[G, foot[r]] > val, foot[r], np.arange(C))]
            both = np.concatenate([own[r], decode(guests)], axis=1).astype(BF)
            q = mx_ref.quantize(((own[r] + gcols(both, a).astype(np.float32)) * np.float32(0.5)).astype(BF))
            now[r] = tile([own[r][:, b::4] + np.maximum(mx_ref.matmul(pick(lay[r], np.arange(128 * b, 128 * b + 128)), q), np.float32(0.0)) * np.float32(0.03125) for b in range(4)])
            last[r] = a
    y, oa = np.zeros((N, 128, C), np.float32), np.zeros((N, 8, C), np.float32)
    oc, osc = np.zeros((N, 128, 4 * C), np.uint8), np.zeros((N, 16, C), np.uint8)
    for r in range(N):
        q = mx_ref.quantize(now[r])
        y[r] = mx_ref.matmul(mx_ref.quantize(v[r]), q)
        oa[r] = last[r]
        oc[r], osc[r] = emit(q)
    return {"y": y, "oa": oa, "oc": oc, "osc": osc}

@@ -1,0 +1,411 @@
+from concourse.mybir import dt, AluOpType, ActivationFunctionType
+
+C, L, S, R = 288, 48, 12, 3
+NE = 2 * C
+CB = C + L
+BIG = 1e29
+F32, BF, I32, U16, H = "float32", "bfloat16", "int32", "uint16", "float16"
+CODE, PLANE = "float8_e4m3fn_x4", "uint8"
+A = AluOpType
+AF = ActivationFunctionType
+
+SCRATCH = {}
+
+
+def _sb(names, n, d):
+    for x in names.split():
+        SCRATCH[x] = ("sbuf", [128, n], d)
+
+
+_sb("xin xs yt dg", 4 * C, BF)
+_sb("ut vt", 512, BF)
+_sb("uq up vq", 128, CODE)
+_sb("us ups vs", 128, PLANE)
+_sb("wq", 512, CODE)
+_sb("wp", 512, PLANE)
+_sb("tq0 tq1 tq2 tq3 lq0 lq1 lq2 yq", C, CODE)
+_sb("ts0 ts1 ts2 ts3 ls0 ls1 ls2 ys", C, PLANE)
+_sb("et", 3072, BF)
+_sb("eq", 768, CODE)
+_sb("es", 768, PLANE)
+_sb("halves", 512, BF)
+_sb("fill mk mseg md lef ph fh wlo whi winv", NE, BF)
+_sb("rti iw", 36, I32)
+_sb("fti", 18, I32)
+_sb("x16 x16b", 16, I32)
+_sb("iu", 8, I32)
+_sb("isw", 4, I32)
+_sb("ik ikb", 2, I32)
+_sb("o_rt o_z o_d o_p o_r", 36, U16)
+_sb("o_ft o_ft3 o_a", 18, U16)
+_sb("o_u", 8, U16)
+_sb("o_sw", 4, U16)
+_sb("oe le", 8 * R, U16)
+_sb("m16 t16", 32, F32)
+_sb("kf sgn", 2, F32)
+_sb("tw sa sb2 sd", 36, F32)
+_sb("ab64 u64 v64 w64", 64, F32)
+_sb("wt", 432, BF)
+_sb("wi", C, BF)
+_sb("ss rl", 4 * C, F32)
+_sb("i288 sc1 s2 m1 e1 mo pp th tp vv vv2 yo", C, F32)
+_sb("zq zt ptab tio r12p r12n z", NE, F32)
+_sb("wr mb yf", NE + 16, F32)
+_sb("dw yh", NE, H)
+_sb("de", L, H)
+_sb("gs", L, F32)
+_sb("f4", 4 * C, BF)
+_sb("d4 o4", 4 * C, H)
+_sb("f3 ab f2", 3 * C, BF)
+_sb("d3 d2 o2", 3 * C, H)
+_sb("da", C, H)
+_sb("bw", 4 * CB, BF)
+for _b in range(8):
+    SCRATCH["pb%d" % _b] = ("psum", [128, 512], F32)
+
+LOADS = ["x", "rt", "u", "ft", "wc", "ws", "v"]
+SEMAPHORES = (["cV", "cS", "cP", "cG", "sent", "outY", "outS"] + ["ld_" + k for k in LOADS]
+              + ["at%d" % t for t in range(R)] + ["ae%d" % t for t in range(R)])
+
+
+def rank_program(g, core, T, topo):
+    rank = T.rank_of(core)
+    if rank is None:
+        return
+    N = len(T.cores)
+    queue = {"V": g.vector, "S": g.scalar, "P": g.tensor, "G": g, "Y": g.sync}
+    count = {"cV": 0, "cS": 0, "cP": 0, "cG": 0, "outY": 0, "outS": 0, "sent": 0}
+    known = {e: {} for e in queue}
+    writer, readers = {}, {}
+
+    def need(e, rd, wr):
+        deps = [writer[k] for k in rd.split() + wr.split() if k in writer]
+        for k in wr.split():
+            deps += readers.get(k, [])
+        best = {}
+        for s, n, clock in deps:
+            if n > best.get(s, (0, None))[0]:
+                best[s] = (n, clock)
+        for s, (n, clock) in best.items():
+            covered = any(s2 != s and c2.get(s, 0) >= n for s2, (n2, c2) in best.items())
+            if known[e].get(s, 0) < n and not covered:
+                queue[e].wait_ge(T.sem[s], n)
+        for s, (n, clock) in best.items():
+            for s2, n2 in list(clock.items()) + [(s, n)]:
+                known[e][s2] = max(known[e].get(s2, 0), n2)
+
+    def done(e, s, n, rd, wr):
+        mark = (s, n, dict(known[e]))
+        for k in rd.split():
+            readers.setdefault(k, []).append(mark)
+        for k in wr.split():
+            writer[k] = mark
+            readers[k] = []
+
+    def op(e, rd, wr, call):
+        need(e, rd, wr)
+        s = "c" + e
+        count[s] += 1
+        call().then_inc(T.sem[s], 1)
+        done(e, s, count[s], rd, wr)
+
+    def load(e, name, out, in_, wr):
+        queue[e].dma_start(out, in_).then_inc(T.sem["ld_" + name], 16)
+        done(e, "ld_" + name, 16, "", wr)
+
+    def store(e, out, in_, rd):
+        need(e, rd, "")
+        count["out" + e] += 16
+        queue[e].dma_start(out, in_).then_inc(T.sem["out" + e], 16)
+
+    V, Sc, P = g.vector, g.scalar, g.tensor
+
+    def cp(out, in_, rd, wr):
+        op("V", rd, wr, lambda: V.tensor_copy(out, in_))
+
+    def tt(out, a, b, o, rd, wr):
+        op("V", rd, wr, lambda: V.tensor_tensor(out, a, b, o))
+
+    def ts(out, a, s1, s2, o0, o1, rd, wr):
+        if s2 is None:
+            op("V", rd, wr, lambda: V.tensor_scalar(out, a, s1, None, o0))
+        else:
+            op("V", rd, wr, lambda: V.tensor_scalar(out, a, s1, s2, o0, o1))
+
+    def scan(out, d0, d1, ini, o0, o1, rd, wr):
+        op("V", rd, wr, lambda: V.tensor_tensor_scan(out, d0, d1, ini, o0, o1))
+
+    def ms(out, c, wr):
+        op("V", "", wr, lambda: V.memset(out, c))
+
+    def turn(out, in_, rd, wr):
+        op("V", rd, wr, lambda: V.transpose(out, in_))
+
+    def qz(q, s, in_, rd, wr):
+        op("V", rd, wr, lambda: V.quantize_mx(q, s, in_))
+
+    def act(out, in_, rd, wr, f=AF.Identity, bias=0.0, scale=1.0):
+        op("S", rd, wr, lambda: Sc.activation(out, in_, f, bias=bias, scale=scale))
+
+    def mm(bank, n, lq, ls, rq, rs, rd):
+        k = "pb%d" % bank
+        op("P", rd, k, lambda: P.matmul_mx(T[k][:, 0:n], lq, ls, rq, rs, True, True))
+
+    def iota(out, pat, base, cm, wr, whole=True):
+        if whole:
+            op("G", "", wr, lambda: g.iota(out, pat, base, cm))
+        else:
+            op("G", "", wr, lambda: g.iota(out, pat, base, cm, allow_small_or_imprecise_dtypes=True))
+
+    def etile(i):
+        src, b = ("fill", i) if i < 4 else ("halves", i - 2)
+        op("G", src, "et%d" % i, lambda: g.affine_select(T.et[:, 512 * i:512 * i + 512], T[src][:, 0:512], [[-1, 512]],
+                                                         A.is_equal, 0.0, b, 4))
+
+    def send(t, pairs, sem, rd):
+        dst = T.cores[(rank + 1 + t) % N]
+        rid, pid = topo.addr(dst, core)
+        need("G", rd, "")
+        for out, in_ in pairs:
+            g.remote_dma(out, in_, T.sem[sem], T.sem.sent, pid, rid, topo.mask(core, dst))
+            count["sent"] += len(topo.engines(core, dst))
+
+    def arrival(t):
+        k = len(topo.engines(T.cores[(rank - 1 - t) % N], core))
+        writer["land%d" % t] = ("at%d" % t, 2 * k, {})
+        writer["le%d" % t] = ("ae%d" % t, k, {})
+
+    def ind(buf, a, b, off, c, d):
+        return T[buf][:, a:b].indirect(T[off][:, c:d])
+
+    def unit(i, rq, rs, bank, rd):
+        mm(bank, C, T.eq[:, 128 * i:128 * i + 128], T.es[:, 128 * i:128 * i + 128], rq[:], rs[:], rd)
+
+    def own_window(b):
+        act(T.bw[:, CB * b:CB * b + C], T["pb%d" % b][:, 0:C], "pb%d" % b, "bw%d" % b, scale=0.5)
+
+    sg = T.sgn[:, 0:1]
+    m16, t16a, t16b = T.m16[:, 0:16], T.t16[:, 0:16], T.t16[:, 16:32]
+
+    load("S", "rt", T.rti[:], T.rt[:], "rti")
+    load("Y", "x", T.xin[:], T.x[:], "xin")
+    load("S", "u", T.ut[:], T.u[:], "ut")
+    load("Y", "ft", T.fti[:], T.ft[:], "fti")
+    load("Y", "wc", T.wq[:].bitcast(dt.uint8), T.wc[:], "wq")
+    load("Y", "ws", T.wp[:], T.ws[:], "wp")
+    load("Y", "v", T.vt[:], T.v[:], "vt")
+    for t in range(R):
+        arrival(t)
+
+    iota(T.x16[:], [[1, 16]], 128, -1, "x16")
+    iota(T.ik[:], [[0, 2]], 0, 1, "ik")
+    iota(T.iw[:], [[16, 36]], 0, 0, "iw")
+    iota(T.iu[:], [[16, 8]], 0, 0, "iu")
+    iota(T.isw[:], [[16, 2], [32, 2]], 0, 0, "isw")
+    iota(T.i288[:], [[1, C]], 0, 0, "i288", False)
+    ms(T.wt[:], 0.0, "wt")
+    ts(T.x16b[:], T.x16[:], 15, None, A.bitwise_and, None, "x16", "x16b")
+    ms(T.fill[:], 1.0, "fill")
+    ts(m16, T.x16b[:], 0.0, None, A.is_equal, None, "x16b", "m16")
+    ts(t16b, T.x16b[:], 1.0, 2.0, A.not_equal, A.mult, "x16b", "t16b")
+    ms(T.mk[:], BIG, "mk")
+    ts(T.ikb[:], T.ik[:], 15, None, A.bitwise_and, None, "ik", "ikb")
+    ts(t16a, m16, -1025.0, -1.0, A.mult, A.add, "m16", "t16a")
+    ts(sg, T.m16[:, 15:16], 2.0, -1.0, A.mult, A.add, "m16", "sgn")
+    cp(T.kf[:], T.ikb[:], "ikb", "kf")
+    ms(T.mk[:, S - 1::S], -BIG, "mk")
+    cp(T.o_u[:], T.iu[:], "iu", "o_u")
+    tt(T.md[:, 0:16], t16a, t16b, A.add, "t16a t16b", "md")
+    ts(T.tw[:], T.iw[:], T.kf[:, 0:1], None, A.add, None, "iw kf", "tw")
+    ts(T.o_sw[:], T.isw[:], T.kf[:, 0:1], None, A.add, None, "isw kf", "o_sw")
+    ms(T.mb[:, 0:1], -BIG, "mb0")
+    ms(T.yf[:, 0:1], 0.0, "yf0")
+    ms(T.wr[:, NE:NE + 1], 0.0, "wr0")
+    ms(T.oe[:], 0, "oe0 oe1 oe2")
+    ms(T.ab64[:], 0.0, "ab64")
+    act(T.wt[:, 144:160], m16, "m16 wt", "wt")
+    act(T.wi[:, 0:16], m16, "m16", "wi")
+    for n, k in ((16, 16), (32, 32), (64, 64), (128, 16)):
+        act(T.wt[:, 144 + n:144 + n + k], T.wt[:, 144:144 + k], "wt", "wt", scale=4.0 ** (n // 16))
+        act(T.wi[:, n:n + k], T.wi[:, 0:k], "wi", "wi", scale=0.25 ** (n // 16))
+    act(T.wi[:, 144:C], T.wi[:, 0:144], "wi", "wi")
+    for n, k in ((16, 16), (32, 32)):
+        act(T.md[:, n:n + k], T.md[:, 0:k], "md", "md")
+    etile(0)
+    etile(1)
+
+    cp(T.o_rt[:], T.rti[:], "rti", "o_rt")
+    act(T.wlo[:], ind("wt", 144, 432, "o_rt", 0, 36), "wt o_rt", "wlo")
+    act(T.whi[:], ind("wt", 0, C, "o_rt", 0, 36), "wt o_rt", "whi")
+    ts(T.sa[:], T.rti[:], 144.0, float(NE), A.is_ge, A.mult, "rti", "sa")
+    qz(T.uq[:], T.us[:], T.ut[:], "ut", "uq")
+    tt(T.sb2[:], T.sa[:], T.tw[:], A.add, "sa tw", "sb2")
+    cp(T.up[:].bitcast(dt.uint32), T.uq[:].bitcast(dt.uint32).indirect(T.o_u[:]), "uq o_u", "up")
+    cp(T.o_z[:], T.sb2[:], "sb2", "o_z")
+    cp(T.ups[:], T.us[:].indirect(T.o_u[:]), "uq o_u", "ups")
+
+    for t in range(R):
+        k = "tq%d" % t
+        tq, tsc, lq, lsc = T[k], T["ts%d" % t], T["lq%d" % t], T["ls%d" % t]
+        le, oe, land = "le%d" % t, "oe%d" % t, "land%d" % t
+        first = t == 0
+        qz(tq[:], tsc[:], T.xin[:] if first else T.xs[:], "xin" if first else "xs0 xs1 xs2 xs3", k)
+        send(t, [(lq[:].bitcast(dt.uint8), tq[:].bitcast(dt.uint8)), (lsc[:], tsc[:])], "at%d" % t, k)
+        mm(4, 144, T.up[:], T.ups[:], tq[:, 0:144], tsc[:, 0:144], "up ups " + k)
+        mm(5, 144, T.up[:], T.ups[:], tq[:, 144:C], tsc[:, 144:C], "up ups " + k)
+        if first:
+            iota(T.tio[:], [[1, NE]], 1, 0, "tio", False)
+            etile(2)
+            scan(T.ss[:, 0:NE], T.wlo[:], T.wlo[:], 0.5, A.add, A.max, "wlo", "ssa")
+        else:
+            for b in range(4):
+                unit(b, tq, tsc, b, "eq " + k)
+        cp(T.sc1[:, 0:144], T.pb4[:, 0:144], "pb4", "s1a")
+        act(T.sc1[:, 144:C], T.pb5[:, 0:144], "pb5", "s1b")
+        if first:
+            scan(T.ss[:, NE:2 * NE], T.whi[:], T.whi[:], 0.5, A.add, A.max, "whi", "ssb")
+        cp(T.z[:, 0:C], ind("sc1", 0, C, "o_rt", 0, 18), "s1a s1b o_rt", "za")
+        act(T.z[:, C:NE], ind("sc1", 0, C, "o_rt", 18, 36), "s1a s1b o_rt", "zb")
+        if first:
+            act(T.winv[:], ind("wi", 0, C, "o_rt", 0, 36), "wi o_rt", "winv")
+            act(T.wr[:, 0:NE], ind("i288", 0, C, "o_rt", 0, 36), "i288 o_rt", "wr")
+            act(T.mseg[:], T.fill[:], "fill", "mseg")
+            act(T.mseg[:, 0::16], T.fill[:, 0:36], "fill", "mseg", scale=0.0)
+            act(T.halves[:], T.fill[:, 0:512], "fill", "halves", scale=0.5)
+            for n, w in ((64, 64), (128, 128), (256, 256), (512, 64)):
+                act(T.md[:, n:n + w], T.md[:, 0:w], "md", "md2")
+        else:
+            own_window(0)
+            own_window(1)
+        scan(T.mb[:, 1:NE + 1], T.z[:], T.mk[:], -BIG, A.max, A.min, "za zb mk", "mb")
+        if first:
+            cp(T.o_ft[:], T.fti[:], "fti", "o_ft")
+        tt(T.lef[:], ind("sc1", 0, C, "o_rt", 0, 36), T.mb[:, 0:NE], A.is_le, "s1a s1b o_rt mb mb0", "lef")
+        if first:
+            tt(T.zq[:], ind("ss", 0, 2 * NE, "o_z", 0, 36), T.winv[:], A.mult, "ssa ssb o_z winv", "zq")
+            tt(T.dw[:], ind("i288", 0, C, "o_rt", 0, 36), T.wr[:, 1:NE + 1], A.subtract, "i288 o_rt wr wr0", "dw")
+            turn(T.zt[:], T.zq[:], "zq", "zt")
+            ts(T.dw[:, S - 1::S], T.wr[:, S - 1:NE:S], 1.0, None, A.add, None, "wr", "dw")
+            scan(T.zq[:], T.mseg[:], T.zt[:], 0.0, A.mult, A.add, "mseg zt", "zq")
+        else:
+            act(T.m1[:], ind("mb", 0, NE, "o_p", 18, 36), "mb mb0 o_p", "m1")
+            act(T.e1[:], T.m1[:], "m1", "e1", AF.Abs, 2.0 ** -125, 1.25 * 2.0 ** -24)
+        scan(T.yh[:], T.lef[:], T.dw[:], 0.0, A.mult, A.add, "lef dw", "yh")
+        if first:
+            ts(T.sa[:], T.zq[:, 15::16], 1.5 * 2.0 ** 25, 1.5 * 2.0 ** 25, A.add, A.subtract, "zq", "sa")
+        scan(T.de[:], T.md[:, 0:L], T.yh[:, S - 1::S], sg, A.mult, A.min, "md yh sgn", "de")
+        if first:
+            tt(T.ab64[:, 0:18], T.sa[:, 0::2], T.zq[:, 15::32], A.is_gt, "sa zq ab64", "aba")
+            tt(T.ab64[:, 32:50], T.sa[:, 1::2], T.zq[:, 31::32], A.is_gt, "sa zq ab64", "abb")
+        ts(T.oe[:, 8 * t:8 * t + 3], T.de[:, 15::16], sg, -1.0, A.mult, A.add, "de sgn", oe)
+        send(t, [(T.le[:, 8 * t:8 * t + 4], T.oe[:, 8 * t:8 * t + 4])], "ae%d" % t, oe)
+        act(T.yf[:, 1:NE + 1], T.yh[:], "yh", "yf")
+        mm(6, C, T.up[:], T.ups[:], lq[:], lsc[:], "up ups " + land)
+        if first:
+            iota(T.r12n[:], [[-1, L], [0, S]], -C, 0, "r12n", False)
+            iota(T.r12p[:], [[1, L], [0, S]], 120, 0, "r12p", False)
+            for i in (3, 4, 5):
+                etile(i)
+            act(T.f4[:, 0::4], T.fill[:, 0:C], "fill", "f4s", scale=0.0)
+            act(T.f4[:, 1::2], T.fill[:], "fill", "f4s")
+            act(T.f3[:, 0::3], T.fill[:, 0:C], "fill", "f3s", scale=0.0)
+            act(T.f2[:, 0::3], T.fill[:, 0:C], "fill", "f2s", scale=0.0)
+            act(T.f2[:, 1::3], T.fill[:, 0:C], "fill", "f2s")
+            act(T.s2[:], T.pb6[:, 0:C], "pb6", "s2")
+            turn(T.u64[:], T.ab64[:], "aba abb", "u64")
+            ts(T.o_ft3[:], T.fti[:], 3.0, 2.0, A.mult, A.add, "fti", "o_ft3")
+            ts(T.v64[:], ind("u64", 0, 64, "o_sw", 0, 4), float(C), None, A.mult, None, "u64 o_sw", "v64")
+            qz(T.vq[:], T.vs[:], T.vt[:], "vt", "vq")
+            turn(T.w64[:], T.v64[:], "v64", "w64")
+            tt(T.sd[:, 0::2], T.w64[:, 0:18], T.rti[:, 0::2], A.add, "w64 rti", "sda")
+            tt(T.sd[:, 1::2], T.w64[:, 32:50], T.rti[:, 1::2], A.add, "w64 rti", "sdb")
+            cp(T.o_d[:], T.sd[:], "sda sdb", "o_d")
+            cp(ind("ptab", 0, NE, "o_d", 0, 36), T.tio[:], "tio o_d", "ptab")
+            scan(T.zt[:], T.md[:], T.ptab[:], sg, A.mult, A.min, "md md2 ptab sgn", "zt")
+            ts(T.o_p[:], T.zt[:, 15::16], sg, -1.0, A.mult, A.add, "zt sgn", "o_p")
+            ts(T.sb2[:], T.zt[:, 15::16], sg, -6.5, A.mult, A.add, "zt sgn", "sb2")
+            act(T.m1[:], ind("mb", 0, NE, "o_p", 18, 36), "mb mb0 o_p", "m1")
+            act(T.d3[:, 2::3], ind("r12p", 0, NE, "o_p", 0, 18), "r12p o_p", "d3c")
+            act(T.e1[:], T.m1[:], "m1", "e1", AF.Abs, 2.0 ** -125, 1.25 * 2.0 ** -24)
+            tt(T.d4[:, 3::4], ind("r12n", 0, NE, "o_p", 18, 36), T.i288[:], A.add, "r12n o_p i288", "d4d")
+            ts(T.sa[:], T.sb2[:], 1.0 / S, 1.5 * 2.0 ** 23, A.mult, A.add, "sb2", "sa")
+            qz(T.eq[:, 0:512], T.es[:, 0:512], T.et[:, 0:2048], "et0 et1 et2 et3", "eq")
+            ts(T.o_r[:], T.sa[:], 1.5 * 2.0 ** 23, None, A.subtract, None, "sa", "o_r")
+            for b in range(4):
+                unit(b, tq, tsc, b, "eq " + k)
+            tt(T.d3[:, 1::3], ind("r12p", 0, NE, "o_p", 18, 36), T.d3[:, 2::3], A.subtract, "r12p o_p d3c", "d3b")
+        act(T.d4[:, 0::4], ind("yf", 0, NE, "o_p", 0, 18), "yf yf0 o_p", "d4a")
+        act(T.d4[:, 2::4], ind("yf", 0, NE, "o_p", 18, 36), "yf yf0 o_p", "d4c")
+        act(T.d4[:, 1::4], T.d4[:, 2::4], "d4c", "d4b", scale=-1.0)
+        if not first:
+            act(T.s2[:], T.pb6[:, 0:C], "pb6", "s2")
+        tt(T.f4[:, 2::4], ind("mb", 0, NE, "o_p", 0, 18), T.m1[:], A.is_ge, "mb mb0 o_p m1", "f4")
+        tt(T.pp[:], ind("mb", 0, NE, "o_p", 18, 36), T.e1[:], A.subtract, "mb mb0 o_p e1", "pp")
+        tt(T.mo[:], ind("mb", 0, NE, "o_p", 0, 18), T.m1[:], A.max, "mb mb0 o_p m1", "mo")
+        tt(T.th[:], ind("mb", 0, NE, "o_p", 0, 18), T.pp[:], A.max, "mb mb0 o_p pp", "th")
+        if first:
+            qz(T.eq[:, 512:768], T.es[:, 512:768], T.et[:, 2048:3072], "et4 et5", "eh")
+        scan(T.o4[:], T.f4[:], T.d4[:], 0.0, A.mult, A.add, "f4 f4s d4a d4b d4c d4d", "o4")
+        act(T.d3[:, 0::3], T.o4[:, 3::4], "o4", "d3a")
+        for b, bank in enumerate((7, 4, 5, 6)):
+            unit(b, lq, lsc, bank, "eq " + land)
+            act(T.dg[:, C * b:C * b + C], T["pb%d" % bank][:, 0:C], "pb%d" % bank, "dg%d" % b)
+        for b, bank in ((2, 7), (3, 4)):
+            unit(b + 2, tq, tsc, bank, "eh " + k)
+        if first:
+            own_window(0)
+            own_window(1)
+        cp(T.gs[:], ind("s2", 0, C, "le", 8 * t, 8 * t + 3), "s2 " + le, "gs")
+        tt(T.tp[:], ind("gs", 0, L, "o_r", 18, 36), T.mo[:], A.max, "gs o_r mo", "tp")
+        tt(T.f3[:, 1::3], ind("gs", 0, L, "o_r", 18, 36), T.th[:], A.is_le, "gs o_r th", "f3b")
+        tt(T.vv[:], ind("gs", 0, L, "o_r", 0, 18), T.tp[:], A.max, "gs o_r tp", "vv")
+        tt(T.f3[:, 2::3], ind("gs", 0, L, "o_r", 0, 18), T.tp[:], A.is_lt, "gs o_r tp", "f3c")
+        act(T.vv2[:], T.vv[:], "vv", "vv2")
+        for b in (0, 1):
+            act(T.fh[:, C * b:C * b + C], T["pb%d" % b][:, 0:C], "pb%d" % b, "fh%d" % b, scale=0.5)
+        scan(T.ab[:], T.f3[:], T.d3[:], 0.0, A.mult, A.add, "f3s f3b f3c d3a d3b d3c", "ab")
+        tt(T.f2[:, 2::3], ind("vv", 0, C, "o_ft", 0, 18), T.vv2[:], A.is_gt, "vv vv2 o_ft", "f2")
+        act(T.d2[:, 0::3], ind("ab", 0, 3 * C, "o_ft3", 0, 18), "ab o_ft3", "d2a")
+        ts(T.d2[:, 1::3], T.ab[:, 2::3], -1.0, None, A.mult, None, "ab", "d2b")
+        ts(T.d2[:, 2::3], T.ab[:, 2::3], 169.0, None, A.add, None, "ab", "d2c")
+        for b in range(4):
+            if b >= 2:
+                own_window(b)
+            act(T.bw[:, CB * b + C:CB * b + CB], ind("dg", C * b, C * b + C, "le", 8 * t, 8 * t + 3),
+                "dg%d %s" % (b, le), "bg%d" % b, scale=0.5)
+        scan(T.o2[:], T.f2[:], T.d2[:], 0.0, A.mult, A.add, "f2 f2s d2a d2b d2c", "o2")
+        scan(T.da[:], T.md[:, 0:C], T.o2[:, 2::3], sg, A.mult, A.min, "md md2 o2 sgn", "da")
+        ts(T.o_a[:], T.da[:, 15::16], sg, -1.0, A.mult, A.add, "da sgn", "o_a")
+        for b in (2, 3):
+            act(T.ph[:, C * b - NE:C * b - C], ind("bw", CB * b, CB * b + CB, "o_a", 0, 18),
+                "bw%d bg%d o_a" % (b, b), "ph%d" % b)
+        for b in (0, 1):
+            tt(T.yt[:, b::4], ind("bw", CB * b, CB * b + CB, "o_a", 0, 18), T.fh[:, C * b:C * b + C], A.add,
+               "bw%d bg%d fh%d o_a" % (b, b, b), "yt%d" % b)
+        for b, bank in ((2, 7), (3, 4)):
+            tt(T.yt[:, b::4], T.ph[:, C * b - NE:C * b - C], T["pb%d" % bank][:, 0:C], A.add,
+               "ph%d pb%d" % (b, bank), "yt%d" % b)
+        if t == R - 1:
+            act(T.pp[:], T.o2[:, 2::3], "o2", "pp", bias=-1.0)
+            store("Y", T.oa[:], T.pp[0:128:16, :], "pp")
+        qz(T.yq[:], T.ys[:], T.yt[:], "yt0 yt1 yt2 yt3", "yq")
+        for b, bank in enumerate((5, 6, 7, 4)):
+            mm(bank, C, T.wq[:, 128 * b:128 * b + 128], T.wp[:, 128 * b:128 * b + 128], T.yq[:], T.ys[:], "wq wp yq")
+        for b, bank in enumerate((5, 6, 7, 4)):
+            act(T.rl[:, C * b:C * b + C], T["pb%d" % bank][:, 0:C], "pb%d" % bank, "rl%d" % b, AF.Relu, 0.0, 0.03125)
+            tt(T.xs[:, b::4], T.rl[:, C * b:C * b + C], T["pb%d" % b][:, 0:C], A.add, "rl%d pb%d" % (b, b), "xs%d" % b)
+
+    qz(T.tq3[:], T.ts3[:], T.xs[:], "xs0 xs1 xs2 xs3", "tq3")
+    mm(5, 144, T.vq[:], T.vs[:], T.tq3[:, 0:144], T.ts3[:, 0:144], "vq tq3")
+    mm(6, 144, T.vq[:], T.vs[:], T.tq3[:, 144:C], T.ts3[:, 144:C], "vq tq3")
+    store("Y", T.oc[:], T.tq3[:].bitcast(dt.uint8), "tq3")
+    for q in range(4):
+        store("YS"[q % 2], T.osc[4 * q:4 * q + 4, :], T.ts3[32 * q:32 * q + 4, :], "tq3")
+    cp(T.yo[:, 0:144], T.pb5[:, 0:144], "pb5", "yoa")
+    act(T.yo[:, 144:C], T.pb6[:, 0:144], "pb6", "yob")
+    store("Y", T.y[:, 0:144], T.yo[:, 0:144], "yoa")
+    store("S", T.y[:, 144:C], T.yo[:, 144:C], "yob")
+    for s in ("cG", "sent", "cP", "cV", "cS"):
+        g.wait_ge(T.sem[s], count[s])
+    g.sync.wait_ge(T.sem.outY, count["outY"])
+    g.scalar.wait_ge(T.sem.outS, count["outS"])

@@ -3,7 +3,13 @@ from concourse.mybir import dt, AluOpType, ActivationFunctionType
 C, L, S, R = 288, 48, 12, 3
 NE = 2 * C
 CB = C + L
+HALVES = ((0, 160), (160, C))
 BIG = 1e29
+FOLD = 1024.0
+MID = CB // 2
+ROUND1, ROUND4 = 1.5 * 2.0 ** 23, 1.5 * 2.0 ** 25
+CYCLE, GATHER, SCATTER, LIST_CALL, G_CALL, WAKE = 0.00083, 1.56, 3.5, 0.06, 0.15, 0.2
+DMA_CALL, LOCAL, REMOTE_CALL, REMOTE, TILE, FIRST = 0.1, 1.5, 0.3, 2.2, 5.2, 2.5
 F32, BF, I32, U16, H = "float32", "bfloat16", "int32", "uint16", "float16"
 CODE, PLANE = "float8_e4m3fn_x4", "uint8"
 A = AluOpType
@@ -25,40 +31,40 @@ _sb("wq", 512, CODE)
 _sb("wp", 512, PLANE)
 _sb("tq0 tq1 tq2 tq3 lq0 lq1 lq2 yq", C, CODE)
 _sb("ts0 ts1 ts2 ts3 ls0 ls1 ls2 ys", C, PLANE)
-_sb("et", 3072, BF)
+_sb("fill diag dhalf", 516, BF)
 _sb("eq", 768, CODE)
 _sb("es", 768, PLANE)
-_sb("halves", 512, BF)
-_sb("fill mk mseg md lef ph fh wlo whi winv", NE, BF)
+_sb("mk mseg md lef ph wlo whi winv", NE, BF)
 _sb("rti iw", 36, I32)
 _sb("fti", 18, I32)
-_sb("x16 x16b", 16, I32)
-_sb("iu", 8, I32)
+_sb("x64 x64b", 64, I32)
 _sb("isw", 4, I32)
 _sb("ik ikb", 2, I32)
-_sb("o_rt o_z o_d o_p o_r", 36, U16)
+_sb("o_rt o_z o_d o_p o_r o_s o_l", 36, U16)
 _sb("o_ft o_ft3 o_a", 18, U16)
 _sb("o_u", 8, U16)
 _sb("o_sw", 4, U16)
 _sb("oe le", 8 * R, U16)
-_sb("m16 t16", 32, F32)
-_sb("kf sgn", 2, F32)
-_sb("tw sa sb2 sd", 36, F32)
+_sb("m16", 16, F32)
+_sb("col", 4, F32)
+_sb("tw sa sb2 sd se rr", 36, F32)
+_sb("l0 l1 l2", 72, F32)
 _sb("ab64 u64 v64 w64", 64, F32)
 _sb("wt", 432, BF)
-_sb("wi", C, BF)
+_sb("wi f01", C, BF)
 _sb("ss rl", 4 * C, F32)
-_sb("i288 sc1 s2 m1 e1 mo pp th tp vv vv2 yo", C, F32)
-_sb("zq zt ptab tio r12p r12n z", NE, F32)
-_sb("wr mb yf", NE + 16, F32)
+_sb("sc1 s2 m1 mo tp vv vv2 yo ao", C, F32)
+_sb("fh", 2 * C, BF)
+_sb("zq zt zs zf ptab tio z", NE, F32)
+_sb("mb yf", NE + 16, F32)
+_sb("wr", NE + 2, H)
 _sb("dw yh", NE, H)
 _sb("de", L, H)
-_sb("gs", L, F32)
-_sb("f4", 4 * C, BF)
-_sb("d4 o4", 4 * C, H)
+_sb("ge", L, F32)
+_sb("gw", 2 * L, F32)
 _sb("f3 ab f2", 3 * C, BF)
 _sb("d3 d2 o2", 3 * C, H)
-_sb("da", C, H)
+_sb("da df jg", C, H)
 _sb("bw", 4 * CB, BF)
 for _b in range(8):
     SCRATCH["pb%d" % _b] = ("psum", [128, 512], F32)
@@ -74,338 +80,386 @@ def rank_program(g, core, T, topo):
         return
     N = len(T.cores)
     queue = {"V": g.vector, "S": g.scalar, "P": g.tensor, "G": g, "Y": g.sync}
-    count = {"cV": 0, "cS": 0, "cP": 0, "cG": 0, "outY": 0, "outS": 0, "sent": 0}
-    known = {e: {} for e in queue}
-    writer, readers = {}, {}
+    calls = []
+    seen = {k: [] for k in SCRATCH}
 
-    def need(e, rd, wr):
-        deps = [writer[k] for k in rd.split() + wr.split() if k in writer]
-        for k in wr.split():
-            deps += readers.get(k, [])
-        best = {}
-        for s, n, clock in deps:
-            if n > best.get(s, (0, None))[0]:
-                best[s] = (n, clock)
-        for s, (n, clock) in best.items():
-            covered = any(s2 != s and c2.get(s, 0) >= n for s2, (n2, c2) in best.items())
-            if known[e].get(s, 0) < n and not covered:
-                queue[e].wait_ge(T.sem[s], n)
-        for s, (n, clock) in best.items():
-            for s2, n2 in list(clock.items()) + [(s, n)]:
-                known[e][s2] = max(known[e].get(s2, 0), n2)
+    def v(name, a=0, b=None, s=1):
+        return (name, a, SCRATCH[name][1][1] if b is None else b, s)
 
-    def done(e, s, n, rd, wr):
-        mark = (s, n, dict(known[e]))
-        for k in rd.split():
-            readers.setdefault(k, []).append(mark)
-        for k in wr.split():
-            writer[k] = mark
-            readers[k] = []
+    def ap(x):
+        if not isinstance(x, tuple):
+            return x
+        if len(x) == 2:
+            w = ap(x[0])
+            if SCRATCH[x[0][0]][2] == CODE:
+                w = w.bitcast(dt.uint32)
+            return w.indirect(ap(x[1]))
+        return T[x[0]][:, x[1]:x[2]:x[3]] if x[3] > 1 else T[x[0]][:, x[1]:x[2]]
 
-    def op(e, rd, wr, call):
-        need(e, rd, wr)
-        s = "c" + e
-        count[s] += 1
-        call().then_inc(T.sem[s], 1)
-        done(e, s, count[s], rd, wr)
+    def touched(outs, ins):
+        r = []
+        for xs, w in ((outs, True), (ins, False)):
+            for x in xs:
+                if isinstance(x, tuple):
+                    r += [(x[0], w), (x[1], False)] if len(x) == 2 else [(x, w)]
+        return [(x[0], {0} if SCRATCH[x[0]][0] == "psum" else set(range(x[1], x[2], x[3])), w) for x, w in r]
 
-    def load(e, name, out, in_, wr):
-        queue[e].dma_start(out, in_).then_inc(T.sem["ld_" + name], 16)
-        done(e, "ld_" + name, 16, "", wr)
+    def note(e, outs, ins, issue, busy, sem, adds, late=0.0, after=()):
+        c = {"e": e, "issue": issue, "busy": busy, "sem": sem, "adds": adds, "late": late, "deps": set(after), "i": len(calls)}
+        acc = touched(outs, ins)
+        for name, cols, w in acc:
+            bank = SCRATCH[name][0] == "psum"
+            c["deps"] |= {c2["i"] for cols2, w2, c2 in seen[name] if (w or w2 or (bank and c2["e"] != e)) and cols & cols2}
+        for name, cols, w in acc:
+            if w:
+                seen[name] = [k for k in seen[name] if not k[0] <= cols]
+        for name, cols, w in acc:
+            seen[name].append([cols, w, c])
+        calls.append(c)
+        return c["i"]
 
-    def store(e, out, in_, rd):
-        need(e, rd, "")
-        count["out" + e] += 16
-        queue[e].dma_start(out, in_).then_inc(T.sem["out" + e], 16)
+    def width(x):
+        return 16 * width(x[1]) if len(x) == 2 else len(range(x[1], x[2], x[3]))
+
+    def op(e, outs, ins, call, cycles=1.0):
+        views = [x for x in outs + ins if isinstance(x, tuple)]
+        n = max(width(x) for x in outs)
+        if len(outs[0]) == 2:
+            busy = LIST_CALL + SCATTER * n * CYCLE
+        elif any(len(x) == 2 for x in views):
+            busy = LIST_CALL + GATHER * n * CYCLE
+        else:
+            short = e == "V" and cycles == 1.0 and all(SCRATCH[x[0]][2] in (BF, H, U16) for x in views if width(x) == n)
+            busy = max(64, n * cycles * (0.5 if short else 1.0)) * CYCLE + (G_CALL if e == "G" else 0.0)
+        note(e, outs, ins, lambda: call().then_inc(T.sem["c" + e], 1), busy, "c" + e, 1)
+
+    def raw(x):
+        return ap(x).bitcast(dt.uint8) if SCRATCH[x[0]][2] == CODE else ap(x)
+
+    def load(e, name, out, late, after=()):
+        return note(e, [out], [], lambda: queue[e].dma_start(raw(out), T[name][:]).then_inc(T.sem["ld_" + name], 16),
+                    DMA_CALL, "ld_" + name, 16, late, after)
+
+    def store(e, out, x, rows=None):
+        src = raw(x) if rows is None else T[x[0]][rows, x[1]:x[2]]
+        note(e, [], [x], lambda: queue[e].dma_start(out, src).then_inc(T.sem["out" + e], 16), DMA_CALL, "out" + e, 16, LOCAL)
+
+    def send(t, pairs, sem, late, first=0.0):
+        dst, src = T.cores[(rank + 1 + t) % N], T.cores[(rank - 1 - t) % N]
+        rid, pid = topo.addr(dst, core)
+
+        def issue():
+            for out, a in pairs:
+                g.remote_dma(raw(out), raw(a), T.sem[sem], T.sem.sent, pid, rid, topo.mask(core, dst))
+        i = note("G", [], [a for out, a in pairs], issue, first + REMOTE_CALL * len(pairs), "sent",
+                 len(pairs) * len(topo.engines(core, dst)))
+        note(None, [out for out, a in pairs], [], None, 0.0, sem, len(pairs) * len(topo.engines(src, core)), late, [i])
+
+    def issue_all():
+        users = [[] for c in calls]
+        for c in calls:
+            for d in c["deps"]:
+                users[d].append(c)
+        for c in reversed(calls):
+            c["way"] = c["busy"] + c["late"] + max([WAKE + u["way"] for u in users[c["i"]]] + [0.0])
+            c["left"] = len(c["deps"])
+            c["ready"] = 0.0
+            if c["sem"][:3] == "ld_":
+                c["way"] = 1e3 - c["i"]
+        free = {e: 0.0 for e in list(queue) + [None]}
+        open_, order = [c for c in calls if not c["deps"]], []
+        while open_:
+            now = {e: max(free[e], min(c["ready"] for c in open_ if c["e"] == e)) for e in {c["e"] for c in open_}}
+            e = min(now, key=lambda k: (now[k], str(k)))
+            mine = [c for c in open_ if c["e"] == e]
+            c = max((k for k in mine if k["ready"] <= now[e]), key=lambda k: (k["way"], -k["i"]))
+            for k in sorted(mine, key=lambda k: k["ready"]):
+                if now[e] < k["ready"] < now[e] + c["busy"] and k["way"] > c["way"] and (
+                        max(k["ready"] + k["way"], k["ready"] + k["busy"] + c["way"]) < now[e] + c["busy"] + k["way"] - SLACK):
+                    c = k
+                    break
+            start = max(now[e], c["ready"])
+            if e is not None:
+                free[e] = start + c["busy"]
+            open_.remove(c)
+            order.append(c)
+            for u in users[c["i"]]:
+                u["ready"] = max(u["ready"], start + c["busy"] + c["late"] + (WAKE if u["e"] else 0.0))
+                u["left"] -= 1
+                if not u["left"]:
+                    open_.append(u)
+        count, known = {}, {e: {} for e in queue}
+        for c in order:
+            e = c["e"]
+            count[c["sem"]] = count.get(c["sem"], 0) + c["adds"]
+            c["count"], c["clock"] = count[c["sem"]], {}
+            if e is None:
+                continue
+            best = {}
+            for d in [calls[i] for i in c["deps"]]:
+                if d["count"] > best.get(d["sem"], {"count": 0})["count"]:
+                    best[d["sem"]] = d
+            for s, d in best.items():
+                if known[e].get(s, 0) < d["count"] and not any(k["clock"].get(s, 0) >= d["count"] for k in best.values()):
+                    queue[e].wait_ge(T.sem[s], d["count"])
+            for s, d in best.items():
+                for s2, n2 in list(d["clock"].items()) + [(s, d["count"])]:
+                    known[e][s2] = max(known[e].get(s2, 0), n2)
+            c["clock"] = dict(known[e])
+            c["issue"]()
+        for s in ("cG", "sent", "cP", "cV", "cS"):
+            g.wait_ge(T.sem[s], count[s])
+        g.sync.wait_ge(T.sem.outY, count["outY"])
+        g.scalar.wait_ge(T.sem.outS, count["outS"])
 
     V, Sc, P = g.vector, g.scalar, g.tensor
 
-    def cp(out, in_, rd, wr):
-        op("V", rd, wr, lambda: V.tensor_copy(out, in_))
+    def cp(out, a):
+        o = ap(out).bitcast(dt.uint32) if len(out) == 4 and SCRATCH[out[0]][2] == CODE else ap(out)
+        op("V", [out], [a], lambda: V.tensor_copy(o, ap(a)))
 
-    def tt(out, a, b, o, rd, wr):
-        op("V", rd, wr, lambda: V.tensor_tensor(out, a, b, o))
+    def tt(out, a, b, o):
+        op("V", [out], [a, b], lambda: V.tensor_tensor(ap(out), ap(a), ap(b), o),
+           1.0 if "psum" in (SCRATCH[a[0]][0] if len(a) == 4 else "", SCRATCH[b[0]][0]) else 2.0)
 
-    def ts(out, a, s1, s2, o0, o1, rd, wr):
-        if s2 is None:
-            op("V", rd, wr, lambda: V.tensor_scalar(out, a, s1, None, o0))
+    def ts(out, a, s1, o0, s2=None, o1=None):
+        if o1 is None:
+            op("V", [out], [a, s1], lambda: V.tensor_scalar(ap(out), ap(a), ap(s1), None, o0))
         else:
-            op("V", rd, wr, lambda: V.tensor_scalar(out, a, s1, s2, o0, o1))
+            op("V", [out], [a, s1, s2], lambda: V.tensor_scalar(ap(out), ap(a), ap(s1), ap(s2), o0, o1))
 
-    def scan(out, d0, d1, ini, o0, o1, rd, wr):
-        op("V", rd, wr, lambda: V.tensor_tensor_scan(out, d0, d1, ini, o0, o1))
+    def scan(out, d0, d1, ini, o0, o1):
+        op("V", [out], [d0, d1, ini], lambda: V.tensor_tensor_scan(ap(out), ap(d0), ap(d1), ap(ini), o0, o1))
 
-    def ms(out, c, wr):
-        op("V", "", wr, lambda: V.memset(out, c))
+    def ms(out, c):
+        op("V", [out], [], lambda: V.memset(ap(out), c))
 
-    def turn(out, in_, rd, wr):
-        op("V", rd, wr, lambda: V.transpose(out, in_))
+    def turn(out, a):
+        op("V", [out], [a], lambda: V.transpose(ap(out), ap(a)))
 
-    def qz(q, s, in_, rd, wr):
-        op("V", rd, wr, lambda: V.quantize_mx(q, s, in_))
+    def qz(q, s, a):
+        op("V", [q, s], [a], lambda: V.quantize_mx(ap(q), ap(s), ap(a)), 1.1)
 
-    def act(out, in_, rd, wr, f=AF.Identity, bias=0.0, scale=1.0):
-        op("S", rd, wr, lambda: Sc.activation(out, in_, f, bias=bias, scale=scale))
-
-    def mm(bank, n, lq, ls, rq, rs, rd):
-        k = "pb%d" % bank
-        op("P", rd, k, lambda: P.matmul_mx(T[k][:, 0:n], lq, ls, rq, rs, True, True))
-
-    def iota(out, pat, base, cm, wr, whole=True):
-        if whole:
-            op("G", "", wr, lambda: g.iota(out, pat, base, cm))
+    def act(out, a, f=AF.Identity, bias=0.0, scale=1.0):
+        if f is AF.Copy:
+            op("S", [out], [a], lambda: Sc.activation(ap(out), ap(a), f))
         else:
-            op("G", "", wr, lambda: g.iota(out, pat, base, cm, allow_small_or_imprecise_dtypes=True))
+            op("S", [out], [a, bias, scale], lambda: Sc.activation(ap(out), ap(a), f, bias=ap(bias), scale=ap(scale)))
 
-    def etile(i):
-        src, b = ("fill", i) if i < 4 else ("halves", i - 2)
-        op("G", src, "et%d" % i, lambda: g.affine_select(T.et[:, 512 * i:512 * i + 512], T[src][:, 0:512], [[-1, 512]],
-                                                         A.is_equal, 0.0, b, 4))
+    def pb(bank, n):
+        return v("pb%d" % bank, 0, n)
 
-    def send(t, pairs, sem, rd):
-        dst = T.cores[(rank + 1 + t) % N]
-        rid, pid = topo.addr(dst, core)
-        need("G", rd, "")
-        for out, in_ in pairs:
-            g.remote_dma(out, in_, T.sem[sem], T.sem.sent, pid, rid, topo.mask(core, dst))
-            count["sent"] += len(topo.engines(core, dst))
+    def mm(bank, lq, ls, i, rq, rs, a=0, b=C):
+        x = [v(lq, 128 * i, 128 * i + 128), v(ls, 128 * i, 128 * i + 128), v(rq, a, b), v(rs, a, b)]
+        op("P", [pb(bank, b - a)], x, lambda: P.matmul_mx(ap(pb(bank, b - a)), ap(x[0]), ap(x[1]), ap(x[2]), ap(x[3]), True, True), 0.8)
 
-    def arrival(t):
-        k = len(topo.engines(T.cores[(rank - 1 - t) % N], core))
-        writer["land%d" % t] = ("at%d" % t, 2 * k, {})
-        writer["le%d" % t] = ("ae%d" % t, k, {})
+    def iota(out, pat, base, cm):
+        if SCRATCH[out[0]][2] == I32:
+            op("G", [out], [], lambda: g.iota(ap(out), pat, base, cm), 2.0)
+        else:
+            op("G", [out], [], lambda: g.iota(ap(out), pat, base, cm, allow_small_or_imprecise_dtypes=True), 2.0)
 
-    def ind(buf, a, b, off, c, d):
-        return T[buf][:, a:b].indirect(T[off][:, c:d])
+    sg, sgr, k16 = v("col", 0, 1), v("col", 1, 2), v("col", 2, 3)
 
-    def unit(i, rq, rs, bank, rd):
-        mm(bank, C, T.eq[:, 128 * i:128 * i + 128], T.es[:, 128 * i:128 * i + 128], rq[:], rs[:], rd)
+    def fold(out, a, n, m=0):
+        scan(v(out, m, n), v("md", m, n), a, sg, A.add, A.min)
+        return v(out, 15, n, 16)
 
-    def own_window(b):
-        act(T.bw[:, CB * b:CB * b + C], T["pb%d" % b][:, 0:C], "pb%d" % b, "bw%d" % b, scale=0.5)
+    load("S", "rt", v("rti"), LOCAL)
+    load("S", "u", v("ut"), LOCAL + 1.3)
+    for name, buf, late in (("x", "xin", 1.0), ("ft", "fti", 1.5), ("v", "vt", 2.0), ("wc", "wq", 3.0), ("ws", "wp", 3.0)):
+        load("Y", name, v(buf), LOCAL + late)
 
-    sg = T.sgn[:, 0:1]
-    m16, t16a, t16b = T.m16[:, 0:16], T.t16[:, 0:16], T.t16[:, 16:32]
+    iota(v("x64"), [[0, 4], [1, 16]], 128, -1)
+    iota(v("ik"), [[0, 2]], 0, 1)
+    iota(v("iw"), [[16, 36]], 0, 0)
+    iota(v("isw"), [[16, 2], [32, 2]], 0, 0)
+    iota(v("tio"), [[1, NE]], 0, 0)
+    ts(v("x64b"), v("x64"), 15, A.bitwise_and)
+    ts(v("m16"), v("x64b", 0, 16), 0.0, A.is_equal)
+    ts(v("u64"), v("x64b"), 0.0, A.is_equal, 2 * FOLD, A.mult)
+    ts(v("v64"), v("x64b"), 1.0, A.is_equal, -FOLD, A.mult)
+    tt(v("md", 0, 64), v("u64"), v("v64"), A.add)
+    for n in range(64, NE, 64):
+        act(v("md", n, n + 64), v("md", 0, 64))
+    ts(sg, v("m16", 15, 16), FOLD, A.mult, -FOLD, A.add)
+    ts(sgr, v("m16", 15, 16), FOLD, A.mult, 0.5 * (S - 1) - FOLD, A.add)
+    ts(v("ikb"), v("ik"), 15, A.bitwise_and)
+    cp(k16, v("ikb", 0, 1))
+    cp(v("o_u"), v("iw", 0, 8))
+    ts(v("tw"), v("iw"), k16, A.add)
+    ts(v("o_sw"), v("isw"), k16, A.add)
+    ms(v("fill"), 1.0)
+    ms(v("mk"), BIG)
+    ms(v("mk", S - 1, NE, S), -BIG)
+    ms(v("mseg"), 1.0)
+    ms(v("mseg", 0, NE, 16), 0.0)
+    ms(v("mb", 0, 1), -BIG)
+    ms(v("yf", 0, 1), 0.0)
+    ms(v("wr", NE, NE + 2), 512.0)
+    ms(v("oe"), 0)
+    ms(v("ab64"), 0.0)
+    act(v("f3", 0, 3 * C, 3), v("fill", 0, C), scale=0.0)
+    act(v("f2", 0, 3 * C, 3), v("fill", 0, C), scale=0.0)
+    act(v("f2", 1, 3 * C, 3), v("fill", 0, C))
+    act(v("l0", 0, 72, 2), v("fill", 0, 36), scale=0.0)
+    act(v("l1", 36, 72, 2), v("fill", 0, 18), scale=float(L))
+    ms(v("wt", 0, 144), 0.0)
+    ms(v("wt", C, 432), 0.0)
+    for c in range(9):
+        act(v("wt", 144 + 16 * c, 160 + 16 * c), v("m16"), scale=4.0 ** c)
+        act(v("wi", 16 * c, 16 * c + 16), v("m16"), scale=0.25 ** c)
+    act(v("wi", 144, C), v("wi", 0, 144))
+    op("G", [v("diag")], [v("fill")],
+       lambda: g.affine_select(T.diag[:], T.fill[:], [[-1, 516]], A.is_equal, 0.0, 3, 4), 2.0)
+    act(v("dhalf"), v("diag"), scale=0.5)
+    for i, (src, b) in enumerate([("diag", b) for b in range(4)] + [("dhalf", 2), ("dhalf", 3)]):
+        qz(v("eq", 128 * i, 128 * i + 128), v("es", 128 * i, 128 * i + 128), v(src, 3 - b, 515 - b))
 
-    load("S", "rt", T.rti[:], T.rt[:], "rti")
-    load("Y", "x", T.xin[:], T.x[:], "xin")
-    load("S", "u", T.ut[:], T.u[:], "ut")
-    load("Y", "ft", T.fti[:], T.ft[:], "fti")
-    load("Y", "wc", T.wq[:].bitcast(dt.uint8), T.wc[:], "wq")
-    load("Y", "ws", T.wp[:], T.ws[:], "wp")
-    load("Y", "v", T.vt[:], T.v[:], "vt")
+    qz(v("tq0"), v("ts0"), v("xin"))
+    qz(v("uq"), v("us"), v("ut"))
+    cp(v("up"), (v("uq"), v("o_u")))
+    act(v("ups"), (v("us"), v("o_u")), AF.Copy)
+    qz(v("vq"), v("vs"), v("vt"))
+    mm(4, "up", "ups", 0, "tq0", "ts0", 0, 144)
+    mm(5, "up", "ups", 0, "tq0", "ts0", 144, C)
+    act(v("sc1", 0, 144), pb(4, 144))
+    cp(v("sc1", 144, C), pb(5, 144))
+
+    cp(v("o_rt"), v("rti"))
+    cp(v("o_ft"), v("fti"))
+    ts(v("o_ft3"), v("fti"), 3.0, A.mult, 2.0, A.add)
+    act(v("wr", 0, NE), (v("tio", 0, C), v("o_rt")), bias=512.0)
+    scan(v("dw"), v("wr", 0, NE), v("wr", 1, NE + 1), 0.0, A.max, A.subtract)
+    ts(v("dw", S - 1, NE, S), v("wr", S - 1, NE, S), -512.0, A.add)
+    act(v("wlo"), (v("wt", 144, 432), v("o_rt")))
+    act(v("whi"), (v("wt", 0, C), v("o_rt")))
+    act(v("winv"), (v("wi"), v("o_rt")))
+    ts(v("sa"), v("rti"), 144.0, A.is_ge, float(NE), A.mult)
+    tt(v("sb2"), v("sa"), v("tw"), A.add)
+    cp(v("o_z"), v("sb2"))
+    scan(v("ss", 0, NE), v("wlo"), v("wlo"), 0.5, A.add, A.max)
+    scan(v("ss", NE, 2 * NE), v("whi"), v("whi"), 0.5, A.add, A.max)
+    for a, e in ((0, 320), (320, NE)):
+        tt(v("zq", a, e), (v("ss"), v("o_z", a // 16, e // 16)), v("winv", a, e), A.mult)
+        turn(v("zt", a, e), v("zq", a, e))
+        scan(v("zs", a, e), v("mseg", a, e), v("zt", a, e), 0.0, A.mult, A.add)
+    ts(v("se"), v("zs", 15, NE, 16), ROUND4, A.add, ROUND4, A.subtract)
+    tt(v("ab64", 0, 18), v("se", 0, 36, 2), v("zs", 15, NE, 32), A.is_gt)
+    tt(v("ab64", 32, 50), v("se", 1, 36, 2), v("zs", 31, NE, 32), A.is_gt)
+    turn(v("u64"), v("ab64"))
+    ts(v("v64"), (v("u64"), v("o_sw")), float(C), A.mult)
+    turn(v("w64"), v("v64"))
+    tt(v("sd", 0, 36, 2), v("w64", 0, 18), v("rti", 0, 36, 2), A.add)
+    tt(v("sd", 1, 36, 2), v("w64", 32, 50), v("rti", 1, 36, 2), A.add)
+    cp(v("o_d"), v("sd"))
+    cp((v("ptab"), v("o_d")), v("tio"))
+    pw = fold("zf", v("ptab"), NE)
+    ts(v("o_p"), pw, sg, A.subtract)
+    ts(v("se"), pw, sgr, A.subtract, 1.0 / S, A.mult)
+    ts(v("rr"), v("se"), ROUND1, A.add, ROUND1, A.subtract)
+    ts(v("o_r"), v("se"), ROUND1, A.add, ROUND1, A.subtract)
+    tt(v("l1", 0, 36, 2), v("zf", 15, C, 16), v("zf", C + 15, NE, 16), A.subtract)
+    ts(v("l1", 1, 36, 2), v("zf", C + 15, NE, 16), sg, A.subtract)
+    ts(v("l1", 37, 72, 2), v("se", 18, 36), ROUND1, A.add, ROUND1, A.subtract)
+    tt(v("sa", 0, 18), v("tw", 0, 18), v("rr", 18, 36), A.subtract)
+    tt(v("sa", 18, 36), v("rr", 18, 36), v("rr", 0, 18), A.subtract)
+    ts(v("o_s"), v("sa"), float(L), A.add)
+    act(v("jg"), (v("tio"), v("o_s", 0, 18)), bias=-float(CB))
+    act(v("d3", 1, 3 * C, 3), (v("tio"), v("o_s", 18, 36)), bias=-float(L))
+    act(v("d3", 2, 3 * C, 3), (v("tio"), v("o_r", 0, 18)), bias=float(C - MID))
+
     for t in range(R):
-        arrival(t)
-
-    iota(T.x16[:], [[1, 16]], 128, -1, "x16")
-    iota(T.ik[:], [[0, 2]], 0, 1, "ik")
-    iota(T.iw[:], [[16, 36]], 0, 0, "iw")
-    iota(T.iu[:], [[16, 8]], 0, 0, "iu")
-    iota(T.isw[:], [[16, 2], [32, 2]], 0, 0, "isw")
-    iota(T.i288[:], [[1, C]], 0, 0, "i288", False)
-    ms(T.wt[:], 0.0, "wt")
-    ts(T.x16b[:], T.x16[:], 15, None, A.bitwise_and, None, "x16", "x16b")
-    ms(T.fill[:], 1.0, "fill")
-    ts(m16, T.x16b[:], 0.0, None, A.is_equal, None, "x16b", "m16")
-    ts(t16b, T.x16b[:], 1.0, 2.0, A.not_equal, A.mult, "x16b", "t16b")
-    ms(T.mk[:], BIG, "mk")
-    ts(T.ikb[:], T.ik[:], 15, None, A.bitwise_and, None, "ik", "ikb")
-    ts(t16a, m16, -1025.0, -1.0, A.mult, A.add, "m16", "t16a")
-    ts(sg, T.m16[:, 15:16], 2.0, -1.0, A.mult, A.add, "m16", "sgn")
-    cp(T.kf[:], T.ikb[:], "ikb", "kf")
-    ms(T.mk[:, S - 1::S], -BIG, "mk")
-    cp(T.o_u[:], T.iu[:], "iu", "o_u")
-    tt(T.md[:, 0:16], t16a, t16b, A.add, "t16a t16b", "md")
-    ts(T.tw[:], T.iw[:], T.kf[:, 0:1], None, A.add, None, "iw kf", "tw")
-    ts(T.o_sw[:], T.isw[:], T.kf[:, 0:1], None, A.add, None, "isw kf", "o_sw")
-    ms(T.mb[:, 0:1], -BIG, "mb0")
-    ms(T.yf[:, 0:1], 0.0, "yf0")
-    ms(T.wr[:, NE:NE + 1], 0.0, "wr0")
-    ms(T.oe[:], 0, "oe0 oe1 oe2")
-    ms(T.ab64[:], 0.0, "ab64")
-    act(T.wt[:, 144:160], m16, "m16 wt", "wt")
-    act(T.wi[:, 0:16], m16, "m16", "wi")
-    for n, k in ((16, 16), (32, 32), (64, 64), (128, 16)):
-        act(T.wt[:, 144 + n:144 + n + k], T.wt[:, 144:144 + k], "wt", "wt", scale=4.0 ** (n // 16))
-        act(T.wi[:, n:n + k], T.wi[:, 0:k], "wi", "wi", scale=0.25 ** (n // 16))
-    act(T.wi[:, 144:C], T.wi[:, 0:144], "wi", "wi")
-    for n, k in ((16, 16), (32, 32)):
-        act(T.md[:, n:n + k], T.md[:, 0:k], "md", "md")
-    etile(0)
-    etile(1)
-
-    cp(T.o_rt[:], T.rti[:], "rti", "o_rt")
-    act(T.wlo[:], ind("wt", 144, 432, "o_rt", 0, 36), "wt o_rt", "wlo")
-    act(T.whi[:], ind("wt", 0, C, "o_rt", 0, 36), "wt o_rt", "whi")
-    ts(T.sa[:], T.rti[:], 144.0, float(NE), A.is_ge, A.mult, "rti", "sa")
-    qz(T.uq[:], T.us[:], T.ut[:], "ut", "uq")
-    tt(T.sb2[:], T.sa[:], T.tw[:], A.add, "sa tw", "sb2")
-    cp(T.up[:].bitcast(dt.uint32), T.uq[:].bitcast(dt.uint32).indirect(T.o_u[:]), "uq o_u", "up")
-    cp(T.o_z[:], T.sb2[:], "sb2", "o_z")
-    cp(T.ups[:], T.us[:].indirect(T.o_u[:]), "uq o_u", "ups")
-
-    for t in range(R):
-        k = "tq%d" % t
-        tq, tsc, lq, lsc = T[k], T["ts%d" % t], T["lq%d" % t], T["ls%d" % t]
-        le, oe, land = "le%d" % t, "oe%d" % t, "land%d" % t
-        first = t == 0
-        qz(tq[:], tsc[:], T.xin[:] if first else T.xs[:], "xin" if first else "xs0 xs1 xs2 xs3", k)
-        send(t, [(lq[:].bitcast(dt.uint8), tq[:].bitcast(dt.uint8)), (lsc[:], tsc[:])], "at%d" % t, k)
-        mm(4, 144, T.up[:], T.ups[:], tq[:, 0:144], tsc[:, 0:144], "up ups " + k)
-        mm(5, 144, T.up[:], T.ups[:], tq[:, 144:C], tsc[:, 144:C], "up ups " + k)
-        if first:
-            iota(T.tio[:], [[1, NE]], 1, 0, "tio", False)
-            etile(2)
-            scan(T.ss[:, 0:NE], T.wlo[:], T.wlo[:], 0.5, A.add, A.max, "wlo", "ssa")
-        else:
-            for b in range(4):
-                unit(b, tq, tsc, b, "eq " + k)
-        cp(T.sc1[:, 0:144], T.pb4[:, 0:144], "pb4", "s1a")
-        act(T.sc1[:, 144:C], T.pb5[:, 0:144], "pb5", "s1b")
-        if first:
-            scan(T.ss[:, NE:2 * NE], T.whi[:], T.whi[:], 0.5, A.add, A.max, "whi", "ssb")
-        cp(T.z[:, 0:C], ind("sc1", 0, C, "o_rt", 0, 18), "s1a s1b o_rt", "za")
-        act(T.z[:, C:NE], ind("sc1", 0, C, "o_rt", 18, 36), "s1a s1b o_rt", "zb")
-        if first:
-            act(T.winv[:], ind("wi", 0, C, "o_rt", 0, 36), "wi o_rt", "winv")
-            act(T.wr[:, 0:NE], ind("i288", 0, C, "o_rt", 0, 36), "i288 o_rt", "wr")
-            act(T.mseg[:], T.fill[:], "fill", "mseg")
-            act(T.mseg[:, 0::16], T.fill[:, 0:36], "fill", "mseg", scale=0.0)
-            act(T.halves[:], T.fill[:, 0:512], "fill", "halves", scale=0.5)
-            for n, w in ((64, 64), (128, 128), (256, 256), (512, 64)):
-                act(T.md[:, n:n + w], T.md[:, 0:w], "md", "md2")
-        else:
-            own_window(0)
-            own_window(1)
-        scan(T.mb[:, 1:NE + 1], T.z[:], T.mk[:], -BIG, A.max, A.min, "za zb mk", "mb")
-        if first:
-            cp(T.o_ft[:], T.fti[:], "fti", "o_ft")
-        tt(T.lef[:], ind("sc1", 0, C, "o_rt", 0, 36), T.mb[:, 0:NE], A.is_le, "s1a s1b o_rt mb mb0", "lef")
-        if first:
-            tt(T.zq[:], ind("ss", 0, 2 * NE, "o_z", 0, 36), T.winv[:], A.mult, "ssa ssb o_z winv", "zq")
-            tt(T.dw[:], ind("i288", 0, C, "o_rt", 0, 36), T.wr[:, 1:NE + 1], A.subtract, "i288 o_rt wr wr0", "dw")
-            turn(T.zt[:], T.zq[:], "zq", "zt")
-            ts(T.dw[:, S - 1::S], T.wr[:, S - 1:NE:S], 1.0, None, A.add, None, "wr", "dw")
-            scan(T.zq[:], T.mseg[:], T.zt[:], 0.0, A.mult, A.add, "mseg zt", "zq")
-        else:
-            act(T.m1[:], ind("mb", 0, NE, "o_p", 18, 36), "mb mb0 o_p", "m1")
-            act(T.e1[:], T.m1[:], "m1", "e1", AF.Abs, 2.0 ** -125, 1.25 * 2.0 ** -24)
-        scan(T.yh[:], T.lef[:], T.dw[:], 0.0, A.mult, A.add, "lef dw", "yh")
-        if first:
-            ts(T.sa[:], T.zq[:, 15::16], 1.5 * 2.0 ** 25, 1.5 * 2.0 ** 25, A.add, A.subtract, "zq", "sa")
-        scan(T.de[:], T.md[:, 0:L], T.yh[:, S - 1::S], sg, A.mult, A.min, "md yh sgn", "de")
-        if first:
-            tt(T.ab64[:, 0:18], T.sa[:, 0::2], T.zq[:, 15::32], A.is_gt, "sa zq ab64", "aba")
-            tt(T.ab64[:, 32:50], T.sa[:, 1::2], T.zq[:, 31::32], A.is_gt, "sa zq ab64", "abb")
-        ts(T.oe[:, 8 * t:8 * t + 3], T.de[:, 15::16], sg, -1.0, A.mult, A.add, "de sgn", oe)
-        send(t, [(T.le[:, 8 * t:8 * t + 4], T.oe[:, 8 * t:8 * t + 4])], "ae%d" % t, oe)
-        act(T.yf[:, 1:NE + 1], T.yh[:], "yh", "yf")
-        mm(6, C, T.up[:], T.ups[:], lq[:], lsc[:], "up ups " + land)
-        if first:
-            iota(T.r12n[:], [[-1, L], [0, S]], -C, 0, "r12n", False)
-            iota(T.r12p[:], [[1, L], [0, S]], 120, 0, "r12p", False)
-            for i in (3, 4, 5):
-                etile(i)
-            act(T.f4[:, 0::4], T.fill[:, 0:C], "fill", "f4s", scale=0.0)
-            act(T.f4[:, 1::2], T.fill[:], "fill", "f4s")
-            act(T.f3[:, 0::3], T.fill[:, 0:C], "fill", "f3s", scale=0.0)
-            act(T.f2[:, 0::3], T.fill[:, 0:C], "fill", "f2s", scale=0.0)
-            act(T.f2[:, 1::3], T.fill[:, 0:C], "fill", "f2s")
-            act(T.s2[:], T.pb6[:, 0:C], "pb6", "s2")
-            turn(T.u64[:], T.ab64[:], "aba abb", "u64")
-            ts(T.o_ft3[:], T.fti[:], 3.0, 2.0, A.mult, A.add, "fti", "o_ft3")
-            ts(T.v64[:], ind("u64", 0, 64, "o_sw", 0, 4), float(C), None, A.mult, None, "u64 o_sw", "v64")
-            qz(T.vq[:], T.vs[:], T.vt[:], "vt", "vq")
-            turn(T.w64[:], T.v64[:], "v64", "w64")
-            tt(T.sd[:, 0::2], T.w64[:, 0:18], T.rti[:, 0::2], A.add, "w64 rti", "sda")
-            tt(T.sd[:, 1::2], T.w64[:, 32:50], T.rti[:, 1::2], A.add, "w64 rti", "sdb")
-            cp(T.o_d[:], T.sd[:], "sda sdb", "o_d")
-            cp(ind("ptab", 0, NE, "o_d", 0, 36), T.tio[:], "tio o_d", "ptab")
-            scan(T.zt[:], T.md[:], T.ptab[:], sg, A.mult, A.min, "md md2 ptab sgn", "zt")
-            ts(T.o_p[:], T.zt[:, 15::16], sg, -1.0, A.mult, A.add, "zt sgn", "o_p")
-            ts(T.sb2[:], T.zt[:, 15::16], sg, -6.5, A.mult, A.add, "zt sgn", "sb2")
-            act(T.m1[:], ind("mb", 0, NE, "o_p", 18, 36), "mb mb0 o_p", "m1")
-            act(T.d3[:, 2::3], ind("r12p", 0, NE, "o_p", 0, 18), "r12p o_p", "d3c")
-            act(T.e1[:], T.m1[:], "m1", "e1", AF.Abs, 2.0 ** -125, 1.25 * 2.0 ** -24)
-            tt(T.d4[:, 3::4], ind("r12n", 0, NE, "o_p", 18, 36), T.i288[:], A.add, "r12n o_p i288", "d4d")
-            ts(T.sa[:], T.sb2[:], 1.0 / S, 1.5 * 2.0 ** 23, A.mult, A.add, "sb2", "sa")
-            qz(T.eq[:, 0:512], T.es[:, 0:512], T.et[:, 0:2048], "et0 et1 et2 et3", "eq")
-            ts(T.o_r[:], T.sa[:], 1.5 * 2.0 ** 23, None, A.subtract, None, "sa", "o_r")
-            for b in range(4):
-                unit(b, tq, tsc, b, "eq " + k)
-            tt(T.d3[:, 1::3], ind("r12p", 0, NE, "o_p", 18, 36), T.d3[:, 2::3], A.subtract, "r12p o_p d3c", "d3b")
-        act(T.d4[:, 0::4], ind("yf", 0, NE, "o_p", 0, 18), "yf yf0 o_p", "d4a")
-        act(T.d4[:, 2::4], ind("yf", 0, NE, "o_p", 18, 36), "yf yf0 o_p", "d4c")
-        act(T.d4[:, 1::4], T.d4[:, 2::4], "d4c", "d4b", scale=-1.0)
-        if not first:
-            act(T.s2[:], T.pb6[:, 0:C], "pb6", "s2")
-        tt(T.f4[:, 2::4], ind("mb", 0, NE, "o_p", 0, 18), T.m1[:], A.is_ge, "mb mb0 o_p m1", "f4")
-        tt(T.pp[:], ind("mb", 0, NE, "o_p", 18, 36), T.e1[:], A.subtract, "mb mb0 o_p e1", "pp")
-        tt(T.mo[:], ind("mb", 0, NE, "o_p", 0, 18), T.m1[:], A.max, "mb mb0 o_p m1", "mo")
-        tt(T.th[:], ind("mb", 0, NE, "o_p", 0, 18), T.pp[:], A.max, "mb mb0 o_p pp", "th")
-        if first:
-            qz(T.eq[:, 512:768], T.es[:, 512:768], T.et[:, 2048:3072], "et4 et5", "eh")
-        scan(T.o4[:], T.f4[:], T.d4[:], 0.0, A.mult, A.add, "f4 f4s d4a d4b d4c d4d", "o4")
-        act(T.d3[:, 0::3], T.o4[:, 3::4], "o4", "d3a")
-        for b, bank in enumerate((7, 4, 5, 6)):
-            unit(b, lq, lsc, bank, "eq " + land)
-            act(T.dg[:, C * b:C * b + C], T["pb%d" % bank][:, 0:C], "pb%d" % bank, "dg%d" % b)
-        for b, bank in ((2, 7), (3, 4)):
-            unit(b + 2, tq, tsc, bank, "eh " + k)
-        if first:
-            own_window(0)
-            own_window(1)
-        cp(T.gs[:], ind("s2", 0, C, "le", 8 * t, 8 * t + 3), "s2 " + le, "gs")
-        tt(T.tp[:], ind("gs", 0, L, "o_r", 18, 36), T.mo[:], A.max, "gs o_r mo", "tp")
-        tt(T.f3[:, 1::3], ind("gs", 0, L, "o_r", 18, 36), T.th[:], A.is_le, "gs o_r th", "f3b")
-        tt(T.vv[:], ind("gs", 0, L, "o_r", 0, 18), T.tp[:], A.max, "gs o_r tp", "vv")
-        tt(T.f3[:, 2::3], ind("gs", 0, L, "o_r", 0, 18), T.tp[:], A.is_lt, "gs o_r tp", "f3c")
-        act(T.vv2[:], T.vv[:], "vv", "vv2")
-        for b in (0, 1):
-            act(T.fh[:, C * b:C * b + C], T["pb%d" % b][:, 0:C], "pb%d" % b, "fh%d" % b, scale=0.5)
-        scan(T.ab[:], T.f3[:], T.d3[:], 0.0, A.mult, A.add, "f3s f3b f3c d3a d3b d3c", "ab")
-        tt(T.f2[:, 2::3], ind("vv", 0, C, "o_ft", 0, 18), T.vv2[:], A.is_gt, "vv vv2 o_ft", "f2")
-        act(T.d2[:, 0::3], ind("ab", 0, 3 * C, "o_ft3", 0, 18), "ab o_ft3", "d2a")
-        ts(T.d2[:, 1::3], T.ab[:, 2::3], -1.0, None, A.mult, None, "ab", "d2b")
-        ts(T.d2[:, 2::3], T.ab[:, 2::3], 169.0, None, A.add, None, "ab", "d2c")
+        tq, tsc, lq, lsc = "tq%d" % t, "ts%d" % t, "lq%d" % t, "ls%d" % t
+        nq, nsc = "tq%d" % (t + 1), "ts%d" % (t + 1)
+        le = v("le", 8 * t, 8 * t + 3)
+        last = t == R - 1
+        send(t, [(v(lq), v(tq)), (v(lsc), v(tsc))], "at%d" % t, TILE, FIRST if t == 0 else 0.0)
         for b in range(4):
-            if b >= 2:
-                own_window(b)
-            act(T.bw[:, CB * b + C:CB * b + CB], ind("dg", C * b, C * b + C, "le", 8 * t, 8 * t + 3),
-                "dg%d %s" % (b, le), "bg%d" % b, scale=0.5)
-        scan(T.o2[:], T.f2[:], T.d2[:], 0.0, A.mult, A.add, "f2 f2s d2a d2b d2c", "o2")
-        scan(T.da[:], T.md[:, 0:C], T.o2[:, 2::3], sg, A.mult, A.min, "md md2 o2 sgn", "da")
-        ts(T.o_a[:], T.da[:, 15::16], sg, -1.0, A.mult, A.add, "da sgn", "o_a")
-        for b in (2, 3):
-            act(T.ph[:, C * b - NE:C * b - C], ind("bw", CB * b, CB * b + CB, "o_a", 0, 18),
-                "bw%d bg%d o_a" % (b, b), "ph%d" % b)
+            mm(b, "eq", "es", b, tq, tsc)
+            act(v("bw", CB * b, CB * b + C), pb(b, C), scale=0.5)
         for b in (0, 1):
-            tt(T.yt[:, b::4], ind("bw", CB * b, CB * b + CB, "o_a", 0, 18), T.fh[:, C * b:C * b + C], A.add,
-               "bw%d bg%d fh%d o_a" % (b, b, b), "yt%d" % b)
-        for b, bank in ((2, 7), (3, 4)):
-            tt(T.yt[:, b::4], T.ph[:, C * b - NE:C * b - C], T["pb%d" % bank][:, 0:C], A.add,
-               "ph%d pb%d" % (b, bank), "yt%d" % b)
-        if t == R - 1:
-            act(T.pp[:], T.o2[:, 2::3], "o2", "pp", bias=-1.0)
-            store("Y", T.oa[:], T.pp[0:128:16, :], "pp")
-        qz(T.yq[:], T.ys[:], T.yt[:], "yt0 yt1 yt2 yt3", "yq")
-        for b, bank in enumerate((5, 6, 7, 4)):
-            mm(bank, C, T.wq[:, 128 * b:128 * b + 128], T.wp[:, 128 * b:128 * b + 128], T.yq[:], T.ys[:], "wq wp yq")
-        for b, bank in enumerate((5, 6, 7, 4)):
-            act(T.rl[:, C * b:C * b + C], T["pb%d" % bank][:, 0:C], "pb%d" % bank, "rl%d" % b, AF.Relu, 0.0, 0.03125)
-            tt(T.xs[:, b::4], T.rl[:, C * b:C * b + C], T["pb%d" % b][:, 0:C], A.add, "rl%d pb%d" % (b, b), "xs%d" % b)
-
-    qz(T.tq3[:], T.ts3[:], T.xs[:], "xs0 xs1 xs2 xs3", "tq3")
-    mm(5, 144, T.vq[:], T.vs[:], T.tq3[:, 0:144], T.ts3[:, 0:144], "vq tq3")
-    mm(6, 144, T.vq[:], T.vs[:], T.tq3[:, 144:C], T.ts3[:, 144:C], "vq tq3")
-    store("Y", T.oc[:], T.tq3[:].bitcast(dt.uint8), "tq3")
+            act(v("fh", C * b, C * b + C), pb(b, C), scale=0.5)
+        cp(v("z", 0, C), (v("sc1"), v("o_rt", 0, 18)))
+        act(v("z", C, NE), (v("sc1"), v("o_rt", 18, 36)))
+        for a, e in ((0, C), (C, NE)):
+            scan(v("mb", a + 1, e + 1), v("z", a, e), v("mk", a, e), -BIG, A.max, A.min)
+        for a, e in ((0, C), (C, NE)):
+            tt(v("lef", a, e), (v("sc1"), v("o_rt", a // 16, e // 16)), v("mb", a, e), A.is_le)
+            scan(v("yh", a, e), v("lef", a, e), v("dw", a, e), 0.0, A.mult, A.add)
+            act(v("yf", a + 1, e + 1), v("yh", a, e))
+        ts(v("oe", 8 * t, 8 * t + 3), fold("de", v("yh", S - 1, NE, S), L), sg, A.subtract)
+        send(t, [(v("le", 8 * t, 8 * t + 4), v("oe", 8 * t, 8 * t + 4))], "ae%d" % t, REMOTE)
+        act(v("m1"), (v("mb", 0, NE), v("o_p", 18, 36)))
+        for a, e in HALVES:
+            tt(v("f01", a, e), (v("mb", 0, NE), v("o_p", a // 16, e // 16)), v("m1", a, e), A.is_ge)
+        fw = fold("df", v("f01"), C)
+        ts(v("l0", 1, 36, 2), fw, sg, A.subtract)
+        ts(v("l0", 37, 72, 2), fw, sg, A.subtract)
+        scan(v("l2"), v("l0"), v("l1"), 0.0, A.mult, A.add)
+        cp(v("o_l"), v("l2", 1, 72, 2))
+        act(v("mo"), (v("mb", 0, NE), v("o_l", 0, 18)))
+        tt(v("d3", 0, 3 * C, 3), (v("yf", 0, NE), v("o_l", 0, 18)), v("jg"), A.add)
+        mm(6, "up", "ups", 0, lq, lsc, 0, 144)
+        mm(7, "up", "ups", 0, lq, lsc, 144, C)
+        cp(v("s2", 0, 144), pb(6, 144))
+        act(v("s2", 144, C), pb(7, 144))
+        for b, bank in enumerate((4, 5, 6, 7)):
+            mm(bank, "eq", "es", b, lq, lsc)
+            act(v("dg", C * b, C * b + C), pb(bank, C))
+        for b in (2, 3):
+            mm(b + 2, "eq", "es", b + 2, tq, tsc)
+        gs, r0, r1 = v("gw", 0, L), v("o_r", 0, 18), v("o_r", 18, 36)
+        cp(gs, (v("s2"), le))
+        act(v("ge"), gs, AF.Abs, 2.0 ** -125, 1.25 * 2.0 ** -24)
+        tt(v("gw", L, 2 * L), gs, v("ge"), A.subtract)
+        for b in range(4):
+            act(v("bw", CB * b + C, CB * b + CB), (v("dg", C * b, C * b + C), le), scale=0.5)
+        tt(v("tp"), (gs, r1), v("mo"), A.max)
+        tt(v("f3", 1, 3 * C, 3), (v("gw"), v("o_l", 18, 36)), v("mo"), A.is_lt)
+        tt(v("f3", 2, 3 * C, 3), (gs, r0), v("tp"), A.is_lt)
+        tt(v("vv"), (gs, r0), v("tp"), A.max)
+        act(v("vv2"), v("vv"))
+        scan(v("ab"), v("f3"), v("d3"), 0.0, A.mult, A.add)
+        act(v("d2", 0, 3 * C, 3), (v("ab"), v("o_ft3")))
+        tt(v("f2", 2, 3 * C, 3), (v("vv"), v("o_ft")), v("vv2"), A.is_gt)
+        ts(v("d2", 1, 3 * C, 3), v("ab", 2, 3 * C, 3), -1.0, A.mult)
+        ts(v("d2", 2, 3 * C, 3), v("ab", 2, 3 * C, 3), float(MID), A.add)
+        for a, e in HALVES:
+            scan(v("o2", 3 * a, 3 * e), v("f2", 3 * a, 3 * e), v("d2", 3 * a, 3 * e), 0.0, A.mult, A.add)
+            fold("da", v("o2", 3 * a + 2, 3 * e, 3), e, a)
+            ts(v("o_a", a // 16, e // 16), v("da", a + 15, e, 16), sg, A.subtract)
+        if last:
+            act(v("ao"), v("o2", 2, 3 * C, 3))
+            store("Y", T.oa[:], v("ao"), slice(0, 128, 16))
+        for h, (a, e) in enumerate(HALVES):
+            for b in (2, 3):
+                act(v("ph", C * b - NE + a, C * b - NE + e), (v("bw", CB * b, CB * b + CB), v("o_a", a // 16, e // 16)))
+                tt(v("yt", 4 * a + b, 4 * e, 4), v("ph", C * b - NE + a, C * b - NE + e), v("pb%d" % (b + 2), a, e), A.add)
+            for b in (0, 1):
+                tt(v("yt", 4 * a + b, 4 * e, 4), (v("bw", CB * b, CB * b + CB), v("o_a", a // 16, e // 16)),
+                   v("fh", C * b + a, C * b + e), A.add)
+            qz(v("yq", a, e), v("ys", a, e), v("yt", 4 * a, 4 * e))
+        for h, (a, e) in enumerate(HALVES):
+            for b, bank in enumerate((6, 7, 4, 5)):
+                mm(bank, "wq", "wp", b, "yq", "ys", a, e)
+                act(v("rl", C * b + a, C * b + e), pb(bank, e - a), AF.Relu, 0.0, 0.03125)
+        for h, (a, e) in enumerate(HALVES):
+            for b in range(4):
+                tt(v("xs", 4 * a + b, 4 * e, 4), v("rl", C * b + a, C * b + e), v("pb%d" % b, a, e), A.add)
+            qz(v(nq, a, e), v(nsc, a, e), v("xs", 4 * a, 4 * e))
+            q, s, out = ("vq", "vs", "yo") if last else ("up", "ups", "sc1")
+            mm(6 + h, q, s, 0, nq, nsc, a, e)
+            if h == 0:
+                act(v(out, a, e), pb(6, e - a))
+            else:
+                cp(v(out, a, e), pb(7, e - a))
+            if last:
+                store("Y", T.oc[:, 4 * a:4 * e], v(nq, a, e))
+                store("SY"[h], T.y[:, a:e], v("yo", a, e))
     for q in range(4):
-        store("YS"[q % 2], T.osc[4 * q:4 * q + 4, :], T.ts3[32 * q:32 * q + 4, :], "tq3")
-    cp(T.yo[:, 0:144], T.pb5[:, 0:144], "pb5", "yoa")
-    act(T.yo[:, 144:C], T.pb6[:, 0:144], "pb6", "yob")
-    store("Y", T.y[:, 0:144], T.yo[:, 0:144], "yoa")
-    store("S", T.y[:, 144:C], T.yo[:, 144:C], "yob")
-    for s in ("cG", "sent", "cP", "cV", "cS"):
-        g.wait_ge(T.sem[s], count[s])
-    g.sync.wait_ge(T.sem.outY, count["outY"])
-    g.scalar.wait_ge(T.sem.outS, count["outS"])
+        store("S", T.osc[4 * q:4 * q + 4, :], v("ts%d" % R), slice(32 * q, 32 * q + 4))
+    issue_all()
+
+
+SLACK = 0.05

@@ -9,7 +9,7 @@ FOLD = 1024.0
 MID = CB // 2
 ROUND1, ROUND4 = 1.5 * 2.0 ** 23, 1.5 * 2.0 ** 25
 CYCLE, GATHER, SCATTER, LIST_CALL, G_CALL, WAKE = 0.00083, 1.56, 3.5, 0.06, 0.15, 0.2
-DMA_CALL, LOCAL, REMOTE_CALL, REMOTE, TILE, FIRST = 0.1, 1.5, 0.3, 2.2, 5.2, 2.5
+DMA_CALL, LOCAL, REMOTE_CALL, REMOTE, COLUMN, FIRST = 0.1, 1.5, 0.3, 2.2, 0.01, 2.5
 F32, BF, I32, U16, H = "float32", "bfloat16", "int32", "uint16", "float16"
 CODE, PLANE = "float8_e4m3fn_x4", "uint8"
 A = AluOpType
@@ -31,7 +31,7 @@ _sb("wq", 512, CODE)
 _sb("wp", 512, PLANE)
 _sb("tq0 tq1 tq2 tq3 lq0 lq1 lq2 yq", C, CODE)
 _sb("ts0 ts1 ts2 ts3 ls0 ls1 ls2 ys", C, PLANE)
-_sb("fill diag dhalf", 516, BF)
+_sb("diag dhalf", 516, BF)
 _sb("eq", 768, CODE)
 _sb("es", 768, PLANE)
 _sb("mk mseg md lef ph wlo whi winv", NE, BF)
@@ -140,20 +140,22 @@ def rank_program(g, core, T, topo):
         return note(e, [out], [], lambda: queue[e].dma_start(raw(out), T[name][:]).then_inc(T.sem["ld_" + name], 16),
                     DMA_CALL, "ld_" + name, 16, late, after)
 
-    def store(e, out, x, rows=None):
+    def store(e, out, x, rows=None, late=LOCAL):
         src = raw(x) if rows is None else T[x[0]][rows, x[1]:x[2]]
-        note(e, [], [x], lambda: queue[e].dma_start(out, src).then_inc(T.sem["out" + e], 16), DMA_CALL, "out" + e, 16, LOCAL)
+        note(e, [], [x], lambda: queue[e].dma_start(out, src).then_inc(T.sem["out" + e], 16), DMA_CALL, "out" + e, 16, late)
 
-    def send(t, pairs, sem, late, first=0.0):
-        dst, src = T.cores[(rank + 1 + t) % N], T.cores[(rank - 1 - t) % N]
+    def send(t, pairs, sem, first=0.0, late=0.0):
+        dst = T.cores[(rank + 1 + t) % N]
         rid, pid = topo.addr(dst, core)
 
         def issue():
             for out, a in pairs:
                 g.remote_dma(raw(out), raw(a), T.sem[sem], T.sem.sent, pid, rid, topo.mask(core, dst))
-        i = note("G", [], [a for out, a in pairs], issue, first + REMOTE_CALL * len(pairs), "sent",
-                 len(pairs) * len(topo.engines(core, dst)))
-        note(None, [out for out, a in pairs], [], None, 0.0, sem, len(pairs) * len(topo.engines(src, core)), late, [i])
+        return note("G", [], [a for out, a in pairs], issue, first + REMOTE_CALL * len(pairs), "sent",
+                    len(pairs) * len(topo.engines(core, dst)), late)
+
+    def arrive(t, outs, sem, writes, late, after):
+        note(None, outs, [], None, 0.0, sem, writes * len(topo.engines(T.cores[(rank - 1 - t) % N], core)), late, after)
 
     def issue_all():
         users = [[] for c in calls]
@@ -173,11 +175,13 @@ def rank_program(g, core, T, topo):
             e = min(now, key=lambda k: (now[k], str(k)))
             mine = [c for c in open_ if c["e"] == e]
             c = max((k for k in mine if k["ready"] <= now[e]), key=lambda k: (k["way"], -k["i"]))
-            for k in sorted(mine, key=lambda k: k["ready"]):
-                if now[e] < k["ready"] < now[e] + c["busy"] and k["way"] > c["way"] and (
-                        max(k["ready"] + k["way"], k["ready"] + k["busy"] + c["way"]) < now[e] + c["busy"] + k["way"] - SLACK):
-                    c = k
-                    break
+            gain, first = SLACK, c
+            for k in mine:
+                at = max(now[e], k["ready"])
+                ahead = max(now[e] + c["way"], max(at, now[e] + c["busy"]) + k["way"]) - max(at + k["way"], at + k["busy"] + c["way"])
+                if ahead > gain:
+                    gain, first = ahead, k
+            c = first
             start = max(now[e], c["ready"])
             if e is not None:
                 free[e] = start + c["busy"]
@@ -246,6 +250,9 @@ def rank_program(g, core, T, topo):
         else:
             op("S", [out], [a, bias, scale], lambda: Sc.activation(ap(out), ap(a), f, bias=ap(bias), scale=ap(scale)))
 
+    def fill(out, c):
+        act(out, v("mseg", 0, width(out)), bias=c, scale=0.0)
+
     def pb(bank, n):
         return v("pb%d" % bank, 0, n)
 
@@ -289,29 +296,28 @@ def rank_program(g, core, T, topo):
     cp(v("o_u"), v("iw", 0, 8))
     ts(v("tw"), v("iw"), k16, A.add)
     ts(v("o_sw"), v("isw"), k16, A.add)
-    ms(v("fill"), 1.0)
-    ms(v("mk"), BIG)
-    ms(v("mk", S - 1, NE, S), -BIG)
     ms(v("mseg"), 1.0)
     ms(v("mseg", 0, NE, 16), 0.0)
+    fill(v("mk"), BIG)
+    fill(v("mk", S - 1, NE, S), -BIG)
     ms(v("mb", 0, 1), -BIG)
     ms(v("yf", 0, 1), 0.0)
     ms(v("wr", NE, NE + 2), 512.0)
     ms(v("oe"), 0)
     ms(v("ab64"), 0.0)
-    act(v("f3", 0, 3 * C, 3), v("fill", 0, C), scale=0.0)
-    act(v("f2", 0, 3 * C, 3), v("fill", 0, C), scale=0.0)
-    act(v("f2", 1, 3 * C, 3), v("fill", 0, C))
-    act(v("l0", 0, 72, 2), v("fill", 0, 36), scale=0.0)
-    act(v("l1", 36, 72, 2), v("fill", 0, 18), scale=float(L))
+    fill(v("f3", 0, 3 * C, 3), 0.0)
+    fill(v("f2", 0, 3 * C, 3), 0.0)
+    fill(v("f2", 1, 3 * C, 3), 1.0)
+    fill(v("l0", 0, 72, 2), 0.0)
+    fill(v("l1", 36, 72, 2), float(L))
     ms(v("wt", 0, 144), 0.0)
     ms(v("wt", C, 432), 0.0)
     for c in range(9):
         act(v("wt", 144 + 16 * c, 160 + 16 * c), v("m16"), scale=4.0 ** c)
         act(v("wi", 16 * c, 16 * c + 16), v("m16"), scale=0.25 ** c)
     act(v("wi", 144, C), v("wi", 0, 144))
-    op("G", [v("diag")], [v("fill")],
-       lambda: g.affine_select(T.diag[:], T.fill[:], [[-1, 516]], A.is_equal, 0.0, 3, 4), 2.0)
+    op("G", [v("diag")], [v("mseg")],
+       lambda: g.affine_select(T.diag[:], T.mseg[:, 0:516], [[-1, 516]], A.is_equal, 0.0, 3, 4), 2.0)
     act(v("dhalf"), v("diag"), scale=0.5)
     for i, (src, b) in enumerate([("diag", b) for b in range(4)] + [("dhalf", 2), ("dhalf", 3)]):
         qz(v("eq", 128 * i, 128 * i + 128), v("es", 128 * i, 128 * i + 128), v(src, 3 - b, 515 - b))
@@ -333,7 +339,7 @@ def rank_program(g, core, T, topo):
     scan(v("dw"), v("wr", 0, NE), v("wr", 1, NE + 1), 0.0, A.max, A.subtract)
     ts(v("dw", S - 1, NE, S), v("wr", S - 1, NE, S), -512.0, A.add)
     act(v("wlo"), (v("wt", 144, 432), v("o_rt")))
-    act(v("whi"), (v("wt", 0, C), v("o_rt")))
+    cp(v("whi"), (v("wt", 0, C), v("o_rt")))
     act(v("winv"), (v("wi"), v("o_rt")))
     ts(v("sa"), v("rti"), 144.0, A.is_ge, float(NE), A.mult)
     tt(v("sb2"), v("sa"), v("tw"), A.add)
@@ -353,9 +359,12 @@ def rank_program(g, core, T, topo):
     tt(v("sd", 0, 36, 2), v("w64", 0, 18), v("rti", 0, 36, 2), A.add)
     tt(v("sd", 1, 36, 2), v("w64", 32, 50), v("rti", 1, 36, 2), A.add)
     cp(v("o_d"), v("sd"))
-    cp((v("ptab"), v("o_d")), v("tio"))
-    pw = fold("zf", v("ptab"), NE)
-    ts(v("o_p"), pw, sg, A.subtract)
+    for a, e in PIECES:
+        cp((v("ptab"), v("o_d", a // 16, e // 16)), v("tio", a, e))
+    for a, e in ((C, NE), (0, C)):
+        fold("zf", v("ptab", a, e), e, a)
+        ts(v("o_p", a // 16, e // 16), v("zf", a + 15, e, 16), sg, A.subtract)
+    pw = v("zf", 15, NE, 16)
     ts(v("se"), pw, sgr, A.subtract, 1.0 / S, A.mult)
     ts(v("rr"), v("se"), ROUND1, A.add, ROUND1, A.subtract)
     ts(v("o_r"), v("se"), ROUND1, A.add, ROUND1, A.subtract)
@@ -374,22 +383,27 @@ def rank_program(g, core, T, topo):
         nq, nsc = "tq%d" % (t + 1), "ts%d" % (t + 1)
         le = v("le", 8 * t, 8 * t + 3)
         last = t == R - 1
-        send(t, [(v(lq), v(tq)), (v(lsc), v(tsc))], "at%d" % t, TILE, FIRST if t == 0 else 0.0)
+        runs = ((0, C),) if t == 0 else HALVES
+        sent = [send(t, [(v(lq, a, e), v(tq, a, e))], "at%d" % t, FIRST if t == 0 else 0.0, (C - a) * COLUMN) for a, e in runs]
+        sent.append(send(t, [(v(lsc), v(tsc))], "at%d" % t))
+        arrive(t, [v(lq), v(lsc)], "at%d" % t, len(sent), REMOTE + C * COLUMN / 4, sent)
         for b in range(4):
             mm(b, "eq", "es", b, tq, tsc)
             act(v("bw", CB * b, CB * b + C), pb(b, C), scale=0.5)
         for b in (0, 1):
             act(v("fh", C * b, C * b + C), pb(b, C), scale=0.5)
-        cp(v("z", 0, C), (v("sc1"), v("o_rt", 0, 18)))
+        for a, e in ((0, 192), (192, C)):
+            cp(v("z", a, e), (v("sc1"), v("o_rt", a // 16, e // 16)))
         act(v("z", C, NE), (v("sc1"), v("o_rt", 18, 36)))
-        for a, e in ((0, C), (C, NE)):
+        for a, e in ((0, 192), (192, C), (C, NE)):
             scan(v("mb", a + 1, e + 1), v("z", a, e), v("mk", a, e), -BIG, A.max, A.min)
         for a, e in ((0, C), (C, NE)):
             tt(v("lef", a, e), (v("sc1"), v("o_rt", a // 16, e // 16)), v("mb", a, e), A.is_le)
             scan(v("yh", a, e), v("lef", a, e), v("dw", a, e), 0.0, A.mult, A.add)
             act(v("yf", a + 1, e + 1), v("yh", a, e))
         ts(v("oe", 8 * t, 8 * t + 3), fold("de", v("yh", S - 1, NE, S), L), sg, A.subtract)
-        send(t, [(v("le", 8 * t, 8 * t + 4), v("oe", 8 * t, 8 * t + 4))], "ae%d" % t, REMOTE)
+        arrive(t, [v("le", 8 * t, 8 * t + 4)], "ae%d" % t, 1, REMOTE,
+               [send(t, [(v("le", 8 * t, 8 * t + 4), v("oe", 8 * t, 8 * t + 4))], "ae%d" % t)])
         act(v("m1"), (v("mb", 0, NE), v("o_p", 18, 36)))
         for a, e in HALVES:
             tt(v("f01", a, e), (v("mb", 0, NE), v("o_p", a // 16, e // 16)), v("m1", a, e), A.is_ge)
@@ -398,7 +412,7 @@ def rank_program(g, core, T, topo):
         ts(v("l0", 37, 72, 2), fw, sg, A.subtract)
         scan(v("l2"), v("l0"), v("l1"), 0.0, A.mult, A.add)
         cp(v("o_l"), v("l2", 1, 72, 2))
-        act(v("mo"), (v("mb", 0, NE), v("o_l", 0, 18)))
+        tt(v("mo"), (v("mb", 0, NE), v("o_p", 0, 18)), v("m1"), A.max)
         tt(v("d3", 0, 3 * C, 3), (v("yf", 0, NE), v("o_l", 0, 18)), v("jg"), A.add)
         mm(6, "up", "ups", 0, lq, lsc, 0, 144)
         mm(7, "up", "ups", 0, lq, lsc, 144, C)
@@ -421,11 +435,11 @@ def rank_program(g, core, T, topo):
         tt(v("vv"), (gs, r0), v("tp"), A.max)
         act(v("vv2"), v("vv"))
         scan(v("ab"), v("f3"), v("d3"), 0.0, A.mult, A.add)
-        act(v("d2", 0, 3 * C, 3), (v("ab"), v("o_ft3")))
-        tt(v("f2", 2, 3 * C, 3), (v("vv"), v("o_ft")), v("vv2"), A.is_gt)
         ts(v("d2", 1, 3 * C, 3), v("ab", 2, 3 * C, 3), -1.0, A.mult)
         ts(v("d2", 2, 3 * C, 3), v("ab", 2, 3 * C, 3), float(MID), A.add)
         for a, e in HALVES:
+            act(v("d2", 3 * a, 3 * e, 3), (v("ab"), v("o_ft3", a // 16, e // 16)))
+            tt(v("f2", 3 * a + 2, 3 * e, 3), (v("vv"), v("o_ft", a // 16, e // 16)), v("vv2", a, e), A.is_gt)
             scan(v("o2", 3 * a, 3 * e), v("f2", 3 * a, 3 * e), v("d2", 3 * a, 3 * e), 0.0, A.mult, A.add)
             fold("da", v("o2", 3 * a + 2, 3 * e, 3), e, a)
             ts(v("o_a", a // 16, e // 16), v("da", a + 15, e, 16), sg, A.subtract)
@@ -455,11 +469,12 @@ def rank_program(g, core, T, topo):
             else:
                 cp(v(out, a, e), pb(7, e - a))
             if last:
-                store("Y", T.oc[:, 4 * a:4 * e], v(nq, a, e))
-                store("SY"[h], T.y[:, a:e], v("yo", a, e))
+                store("Y", T.oc[:, 4 * a:4 * e], v(nq, a, e), None, LOCAL + 1 - h)
+                store("SY"[h], T.y[:, a:e], v("yo", a, e), None, LOCAL + 1 - h)
     for q in range(4):
-        store("S", T.osc[4 * q:4 * q + 4, :], v("ts%d" % R), slice(32 * q, 32 * q + 4))
+        store("SY"[q % 2], T.osc[4 * q:4 * q + 4, :], v("ts%d" % R), slice(32 * q, 32 * q + 4), LOCAL - 0.5)
     issue_all()
 
 
-SLACK = 0.05
+SLACK = 0.15
+PIECES = ((0, C), (C, NE))

@@ -10,6 +10,13 @@ MID = CB // 2
 ROUND1, ROUND4 = 1.5 * 2.0 ** 23, 1.5 * 2.0 ** 25
 CYCLE, GATHER, SCATTER, LIST_CALL, G_CALL, WAKE = 0.00083, 1.56, 3.5, 0.06, 0.15, 0.2
 DMA_CALL, LOCAL, REMOTE_CALL, REMOTE, COLUMN, FIRST = 0.1, 1.5, 0.3, 2.2, 0.01, 2.5
+SLACK = 0.15
+ROUTES_FIRST = ("o_rt sa w64 w64 whi tq0 sb2 uq ss up ss o_z r64 o_ft zq zq zt zt zs zs dw se mb ab64 ab64 mb dw u64 mb lef "
+                "v64 lef w64 lef o_d o_d lef yh eq yh eq de eq oe ptab eq zf zf o_p eq o_p se l1 l1 eq rr o_r l1 o_ft3 "
+                "sa sa f01 o_s f01 mo df gw l0 l0 tp l2 tp o_l gw f3 vv d3 f3 f3")
+ROUTES = "z z mb mb mb lef lef yh yh f01 de f01 oe f01 df vq l0 l0 l2 o_l d3 s2 gw tp tp gw f3 vv f3 f3"
+SOURCES = "ab ab vv2 vv2 f2 f2 o2 o2 o_a o_a"
+LAYER = "yt yt yt yt yt yq yt yt yt yq xs xs xs xs tq xs xs xs xs tq sc1"
 F32, BF, I32, U16, H = "float32", "bfloat16", "int32", "uint16", "float16"
 CODE, PLANE = "float8_e4m3fn_x4", "uint8"
 A = AluOpType
@@ -46,14 +53,14 @@ _sb("o_u", 8, U16)
 _sb("o_sw", 4, U16)
 _sb("oe le", 8 * R, U16)
 _sb("m16", 16, F32)
-_sb("col", 4, F32)
-_sb("tw sa sb2 sd se rr", 36, F32)
+_sb("col", 6, F32)
+_sb("tw sa sb2 se rr", 36, F32)
 _sb("l0 l1 l2", 72, F32)
-_sb("ab64 u64 v64 w64", 64, F32)
+_sb("ab64 u64 v64 w64 r64", 64, F32)
 _sb("wt", 432, BF)
 _sb("wi f01", C, BF)
 _sb("ss rl", 4 * C, F32)
-_sb("sc1 s2 m1 mo tp vv vv2 yo ao", C, F32)
+_sb("sc1 s2 m1 mo tp vv vv2 ao", C, F32)
 _sb("fh", 2 * C, BF)
 _sb("zq zt zs zf ptab tio z", NE, F32)
 _sb("mb yf", NE + 16, F32)
@@ -62,10 +69,14 @@ _sb("dw yh", NE, H)
 _sb("de", L, H)
 _sb("ge", L, F32)
 _sb("gw", 2 * L, F32)
-_sb("f3 ab f2", 3 * C, BF)
-_sb("d3 d2 o2", 3 * C, H)
-_sb("da df jg", C, H)
-_sb("bw", 4 * CB, BF)
+_sb("f3 ab", 3 * C, BF)
+_sb("d3", 3 * C, H)
+_sb("f2", NE, BF)
+_sb("d2 o2", NE, H)
+_sb("own", C, BF)
+_sb("twice", 2 * CB, F32)
+_sb("df jg", C, H)
+_sb("bw", 8 * CB, BF)
 for _b in range(8):
     SCRATCH["pb%d" % _b] = ("psum", [128, 512], F32)
 
@@ -80,6 +91,7 @@ def rank_program(g, core, T, topo):
         return
     N = len(T.cores)
     queue = {"V": g.vector, "S": g.scalar, "P": g.tensor, "G": g, "Y": g.sync}
+    turns = []
     calls = []
     seen = {k: [] for k in SCRATCH}
 
@@ -105,7 +117,8 @@ def rank_program(g, core, T, topo):
         return [(x[0], {0} if SCRATCH[x[0]][0] == "psum" else set(range(x[1], x[2], x[3])), w) for x, w in r]
 
     def note(e, outs, ins, issue, busy, sem, adds, late=0.0, after=()):
-        c = {"e": e, "issue": issue, "busy": busy, "sem": sem, "adds": adds, "late": late, "deps": set(after), "i": len(calls)}
+        c = {"e": e, "issue": issue, "busy": busy, "sem": sem, "adds": adds, "late": late, "deps": set(after), "i": len(calls),
+             "name": (outs[0] if len(outs[0]) == 4 else outs[0][0])[0] if outs else ""}
         acc = touched(outs, ins)
         for name, cols, w in acc:
             bank = SCRATCH[name][0] == "psum"
@@ -158,18 +171,39 @@ def rank_program(g, core, T, topo):
         note(None, outs, [], None, 0.0, sem, writes * len(topo.engines(T.cores[(rank - 1 - t) % N], core)), late, after)
 
     def issue_all():
-        users = [[] for c in calls]
+        users, follows, before = [[] for c in calls], [[] for c in calls], None
         for c in calls:
+            c["left"], c["ready"] = len(c["deps"]), 0.0
             for d in c["deps"]:
                 users[d].append(c)
-        for c in reversed(calls):
-            c["way"] = c["busy"] + c["late"] + max([WAKE + u["way"] for u in users[c["i"]]] + [0.0])
-            c["left"] = len(c["deps"])
-            c["ready"] = 0.0
+        for names, pool in turns:
+            for name in names.split():
+                c = next((k for k in pool if k["e"] == "V" and k["name"] == name), None)
+                if c:
+                    pool.remove(c)
+                    if before:
+                        follows[before["i"]].append(c)
+                        c["left"] += 1
+                    before = c
+        first_list = next(c for c in calls if c["sem"] == "ae0")
+        for c in calls:
+            if c["e"] == "G" and c["name"] == "bw":
+                follows[min(first_list["deps"])].append(c)
+                c["left"] += 1
+        left = [c["left"] for c in calls]
+        ranked = [c for c in calls if not c["left"]]
+        for c in ranked:
+            for u in users[c["i"]] + follows[c["i"]]:
+                left[u["i"]] -= 1
+                if not left[u["i"]]:
+                    ranked.append(u)
+        for c in reversed(ranked):
+            c["way"] = c["busy"] + max([c["late"]] + [c["late"] + WAKE + u["way"] for u in users[c["i"]]]
+                                       + [u["way"] for u in follows[c["i"]]])
             if c["sem"][:3] == "ld_":
                 c["way"] = 1e3 - c["i"]
         free = {e: 0.0 for e in list(queue) + [None]}
-        open_, order = [c for c in calls if not c["deps"]], []
+        open_, order = [c for c in calls if not c["left"]], []
         while open_:
             now = {e: max(free[e], min(c["ready"] for c in open_ if c["e"] == e)) for e in {c["e"] for c in open_}}
             e = min(now, key=lambda k: (now[k], str(k)))
@@ -189,6 +223,7 @@ def rank_program(g, core, T, topo):
             order.append(c)
             for u in users[c["i"]]:
                 u["ready"] = max(u["ready"], start + c["busy"] + c["late"] + (WAKE if u["e"] else 0.0))
+            for u in users[c["i"]] + follows[c["i"]]:
                 u["left"] -= 1
                 if not u["left"]:
                     open_.append(u)
@@ -260,13 +295,16 @@ def rank_program(g, core, T, topo):
         x = [v(lq, 128 * i, 128 * i + 128), v(ls, 128 * i, 128 * i + 128), v(rq, a, b), v(rs, a, b)]
         op("P", [pb(bank, b - a)], x, lambda: P.matmul_mx(ap(pb(bank, b - a)), ap(x[0]), ap(x[1]), ap(x[2]), ap(x[3]), True, True), 0.8)
 
+    def copy(out, a):
+        op("G", [out], [a], lambda: g.affine_select(ap(out), ap(a), [[0, width(out)]], A.is_ge, 0.0, 0, 0), 2.0)
+
     def iota(out, pat, base, cm):
         if SCRATCH[out[0]][2] == I32:
             op("G", [out], [], lambda: g.iota(ap(out), pat, base, cm), 2.0)
         else:
             op("G", [out], [], lambda: g.iota(ap(out), pat, base, cm, allow_small_or_imprecise_dtypes=True), 2.0)
 
-    sg, sgr, k16 = v("col", 0, 1), v("col", 1, 2), v("col", 2, 3)
+    sg, sgr, k16, sgf = [v("col", i, i + 1) for i in range(4)]
 
     def fold(out, a, n, m=0):
         scan(v(out, m, n), v("md", m, n), a, sg, A.add, A.min)
@@ -274,7 +312,7 @@ def rank_program(g, core, T, topo):
 
     load("S", "rt", v("rti"), LOCAL)
     load("S", "u", v("ut"), LOCAL + 1.3)
-    for name, buf, late in (("x", "xin", 1.0), ("ft", "fti", 1.5), ("v", "vt", 2.0), ("wc", "wq", 3.0), ("ws", "wp", 3.0)):
+    for name, buf, late in (("x", "xin", 1.0), ("ft", "fti", 1.5), ("v", "vt", 25.0), ("wc", "wq", 3.0), ("ws", "wp", 3.0)):
         load("Y", name, v(buf), LOCAL + late)
 
     iota(v("x64"), [[0, 4], [1, 16]], 128, -1)
@@ -300,14 +338,19 @@ def rank_program(g, core, T, topo):
     ms(v("mseg", 0, NE, 16), 0.0)
     fill(v("mk"), BIG)
     fill(v("mk", S - 1, NE, S), -BIG)
-    ms(v("mb", 0, 1), -BIG)
+    ms(v("mb", 0, C + 1, 96), -BIG)
     ms(v("yf", 0, 1), 0.0)
     ms(v("wr", NE, NE + 2), 512.0)
     ms(v("oe"), 0)
     ms(v("ab64"), 0.0)
+    ms(v("w64"), 0.0)
     fill(v("f3", 0, 3 * C, 3), 0.0)
-    fill(v("f2", 0, 3 * C, 3), 0.0)
-    fill(v("f2", 1, 3 * C, 3), 1.0)
+    act(v("f2", 0, NE, 2), v("md", 0, C), scale=1 / FOLD)
+    act(v("own"), v("md", 0, C), AF.Relu)
+    act(v("own"), v("own"), bias=BIG, scale=-BIG / FOLD)
+    for w in (0, CB):
+        act(v("twice", w, w + CB), v("tio", 0, CB))
+    ts(sgf, v("m16", 15, 16), -1.0, A.add)
     fill(v("l0", 0, 72, 2), 0.0)
     fill(v("l1", 36, 72, 2), float(L))
     ms(v("wt", 0, 144), 0.0)
@@ -319,6 +362,7 @@ def rank_program(g, core, T, topo):
     op("G", [v("diag")], [v("mseg")],
        lambda: g.affine_select(T.diag[:], T.mseg[:, 0:516], [[-1, 516]], A.is_equal, 0.0, 3, 4), 2.0)
     act(v("dhalf"), v("diag"), scale=0.5)
+    mark = len(calls)
     for i, (src, b) in enumerate([("diag", b) for b in range(4)] + [("dhalf", 2), ("dhalf", 3)]):
         qz(v("eq", 128 * i, 128 * i + 128), v("es", 128 * i, 128 * i + 128), v(src, 3 - b, 515 - b))
 
@@ -326,11 +370,10 @@ def rank_program(g, core, T, topo):
     qz(v("uq"), v("us"), v("ut"))
     cp(v("up"), (v("uq"), v("o_u")))
     act(v("ups"), (v("us"), v("o_u")), AF.Copy)
-    qz(v("vq"), v("vs"), v("vt"))
     mm(4, "up", "ups", 0, "tq0", "ts0", 0, 144)
     mm(5, "up", "ups", 0, "tq0", "ts0", 144, C)
     act(v("sc1", 0, 144), pb(4, 144))
-    cp(v("sc1", 144, C), pb(5, 144))
+    act(v("sc1", 144, C), pb(5, 144))
 
     cp(v("o_rt"), v("rti"))
     cp(v("o_ft"), v("fti"))
@@ -350,19 +393,20 @@ def rank_program(g, core, T, topo):
         tt(v("zq", a, e), (v("ss"), v("o_z", a // 16, e // 16)), v("winv", a, e), A.mult)
         turn(v("zt", a, e), v("zq", a, e))
         scan(v("zs", a, e), v("mseg", a, e), v("zt", a, e), 0.0, A.mult, A.add)
+    ts(v("w64", 0, 18), v("rti", 0, 36, 2), 2.0, A.mult)
+    ts(v("w64", 32, 50), v("rti", 1, 36, 2), 2.0, A.mult)
+    turn(v("r64"), v("w64"))
     ts(v("se"), v("zs", 15, NE, 16), ROUND4, A.add, ROUND4, A.subtract)
     tt(v("ab64", 0, 18), v("se", 0, 36, 2), v("zs", 15, NE, 32), A.is_gt)
     tt(v("ab64", 32, 50), v("se", 1, 36, 2), v("zs", 31, NE, 32), A.is_gt)
     turn(v("u64"), v("ab64"))
-    ts(v("v64"), (v("u64"), v("o_sw")), float(C), A.mult)
+    tt(v("v64"), (v("u64"), v("o_sw")), v("r64"), A.add)
     turn(v("w64"), v("v64"))
-    tt(v("sd", 0, 36, 2), v("w64", 0, 18), v("rti", 0, 36, 2), A.add)
-    tt(v("sd", 1, 36, 2), v("w64", 32, 50), v("rti", 1, 36, 2), A.add)
-    cp(v("o_d"), v("sd"))
-    for a, e in PIECES:
-        cp((v("ptab"), v("o_d", a // 16, e // 16)), v("tio", a, e))
+    cp(v("o_d", 0, 36, 2), v("w64", 0, 18))
+    cp(v("o_d", 1, 36, 2), v("w64", 32, 50))
+    cp((v("ptab"), v("o_d")), v("tio"))
     for a, e in ((C, NE), (0, C)):
-        fold("zf", v("ptab", a, e), e, a)
+        fold("zf", v("ptab", a // C, NE, 2), e, a)
         ts(v("o_p", a // 16, e // 16), v("zf", a + 15, e, 16), sg, A.subtract)
     pw = v("zf", 15, NE, 16)
     ts(v("se"), pw, sgr, A.subtract, 1.0 / S, A.mult)
@@ -389,70 +433,84 @@ def rank_program(g, core, T, topo):
         arrive(t, [v(lq), v(lsc)], "at%d" % t, len(sent), REMOTE + C * COLUMN / 4, sent)
         for b in range(4):
             mm(b, "eq", "es", b, tq, tsc)
-            act(v("bw", CB * b, CB * b + C), pb(b, C), scale=0.5)
+            for w in (2 * b, 2 * b + 1):
+                if t or w % 2 == 0:
+                    act(v("bw", CB * w, CB * w + C), pb(b, C), scale=0.5)
+                else:
+                    copy(v("bw", CB * w, CB * w + C), v("bw", CB * w - CB, CB * w - L))
         for b in (0, 1):
             act(v("fh", C * b, C * b + C), pb(b, C), scale=0.5)
         for a, e in ((0, 192), (192, C)):
-            cp(v("z", a, e), (v("sc1"), v("o_rt", a // 16, e // 16)))
+            (cp if t else act)(v("z", a, e), (v("sc1"), v("o_rt", a // 16, e // 16)))
         act(v("z", C, NE), (v("sc1"), v("o_rt", 18, 36)))
-        for a, e in ((0, 192), (192, C), (C, NE)):
-            scan(v("mb", a + 1, e + 1), v("z", a, e), v("mk", a, e), -BIG, A.max, A.min)
-        for a, e in ((0, C), (C, NE)):
+        for a, e in ((0, 192), (192, C), (C, NE)) if t else ((C, NE), (0, 192), (192, C)):
+            scan(v("mb", a + 1, e), v("z", a, e - 1), v("mk", a, e - 1), -BIG, A.max, A.min)
+        for a, e in ((0, C), (C, NE)) if t else ((416, NE), (C, 416), (0, 128), (128, C)):
             tt(v("lef", a, e), (v("sc1"), v("o_rt", a // 16, e // 16)), v("mb", a, e), A.is_le)
+        for a, e in ((0, C), (C, NE)) if t else ((C, NE), (0, C)):
             scan(v("yh", a, e), v("lef", a, e), v("dw", a, e), 0.0, A.mult, A.add)
             act(v("yf", a + 1, e + 1), v("yh", a, e))
         ts(v("oe", 8 * t, 8 * t + 3), fold("de", v("yh", S - 1, NE, S), L), sg, A.subtract)
         arrive(t, [v("le", 8 * t, 8 * t + 4)], "ae%d" % t, 1, REMOTE,
                [send(t, [(v("le", 8 * t, 8 * t + 4), v("oe", 8 * t, 8 * t + 4))], "ae%d" % t)])
         act(v("m1"), (v("mb", 0, NE), v("o_p", 18, 36)))
-        for a, e in HALVES:
+        for a, e in ((0, 96), (96, 192), (192, C)) if t else HALVES:
             tt(v("f01", a, e), (v("mb", 0, NE), v("o_p", a // 16, e // 16)), v("m1", a, e), A.is_ge)
         fw = fold("df", v("f01"), C)
         ts(v("l0", 1, 36, 2), fw, sg, A.subtract)
         ts(v("l0", 37, 72, 2), fw, sg, A.subtract)
         scan(v("l2"), v("l0"), v("l1"), 0.0, A.mult, A.add)
         cp(v("o_l"), v("l2", 1, 72, 2))
-        tt(v("mo"), (v("mb", 0, NE), v("o_p", 0, 18)), v("m1"), A.max)
+        if t:
+            act(v("mo"), (v("mb", 0, NE), v("o_l", 0, 18)))
+        else:
+            tt(v("mo"), (v("mb", 0, NE), v("o_p", 0, 18)), v("m1"), A.max)
         tt(v("d3", 0, 3 * C, 3), (v("yf", 0, NE), v("o_l", 0, 18)), v("jg"), A.add)
+        if t == 1:
+            qz(v("vq"), v("vs"), v("vt"))
         mm(6, "up", "ups", 0, lq, lsc, 0, 144)
         mm(7, "up", "ups", 0, lq, lsc, 144, C)
-        cp(v("s2", 0, 144), pb(6, 144))
+        (cp if t else act)(v("s2", 0, 144), pb(6, 144))
         act(v("s2", 144, C), pb(7, 144))
         for b, bank in enumerate((4, 5, 6, 7)):
             mm(bank, "eq", "es", b, lq, lsc)
             act(v("dg", C * b, C * b + C), pb(bank, C))
         for b in (2, 3):
             mm(b + 2, "eq", "es", b + 2, tq, tsc)
-        gs, r0, r1 = v("gw", 0, L), v("o_r", 0, 18), v("o_r", 18, 36)
+        gs, r0 = v("gw", 0, L), v("o_r", 0, 18)
         cp(gs, (v("s2"), le))
         act(v("ge"), gs, AF.Abs, 2.0 ** -125, 1.25 * 2.0 ** -24)
         tt(v("gw", L, 2 * L), gs, v("ge"), A.subtract)
-        for b in range(4):
-            act(v("bw", CB * b + C, CB * b + CB), (v("dg", C * b, C * b + C), le), scale=0.5)
-        tt(v("tp"), (gs, r1), v("mo"), A.max)
-        tt(v("f3", 1, 3 * C, 3), (v("gw"), v("o_l", 18, 36)), v("mo"), A.is_lt)
-        tt(v("f3", 2, 3 * C, 3), (gs, r0), v("tp"), A.is_lt)
-        tt(v("vv"), (gs, r0), v("tp"), A.max)
-        act(v("vv2"), v("vv"))
-        scan(v("ab"), v("f3"), v("d3"), 0.0, A.mult, A.add)
-        ts(v("d2", 1, 3 * C, 3), v("ab", 2, 3 * C, 3), -1.0, A.mult)
-        ts(v("d2", 2, 3 * C, 3), v("ab", 2, 3 * C, 3), float(MID), A.add)
+        for w in range(8):
+            act(v("bw", CB * w + C, CB * w + CB), (v("dg", C * (w // 2), C * (w // 2) + C), le), scale=0.5)
         for a, e in HALVES:
-            act(v("d2", 3 * a, 3 * e, 3), (v("ab"), v("o_ft3", a // 16, e // 16)))
-            tt(v("f2", 3 * a + 2, 3 * e, 3), (v("vv"), v("o_ft", a // 16, e // 16)), v("vv2", a, e), A.is_gt)
-            scan(v("o2", 3 * a, 3 * e), v("f2", 3 * a, 3 * e), v("d2", 3 * a, 3 * e), 0.0, A.mult, A.add)
-            fold("da", v("o2", 3 * a + 2, 3 * e, 3), e, a)
-            ts(v("o_a", a // 16, e // 16), v("da", a + 15, e, 16), sg, A.subtract)
+            tt(v("tp", a, e), (gs, v("o_r", 18 + a // 16, 18 + e // 16)), v("mo", a, e), A.max)
+        tt(v("vv"), (gs, r0), v("tp"), A.max)
+        for a, e in HALVES:
+            scan(v("vv2", a, e), v("vv", a, e), v("own", a, e), BIG, A.min, A.max)
+        for a, e in HALVES:
+            tt(v("f3", 3 * a + 2, 3 * e, 3), (gs, v("o_r", a // 16, e // 16)), v("tp", a, e), A.is_lt)
+            if a == 0:
+                tt(v("f3", 1, 3 * C, 3), (v("gw"), v("o_l", 18, 36)), v("mo"), A.is_lt)
+        for a, e in HALVES:
+            scan(v("ab", 3 * a, 3 * e), v("f3", 3 * a, 3 * e), v("d3", 3 * a, 3 * e), 0.0, A.mult, A.add)
+        for a, e in HALVES:
+            act(v("d2", 2 * a, 2 * e, 2), v("ab", 3 * a + 2, 3 * e, 3), bias=MID / FOLD, scale=1 / FOLD)
+            act(v("d2", 2 * a + 1, 2 * e, 2), (v("ab"), v("o_ft3", a // 16, e // 16)), bias=(CB + MID) / FOLD, scale=1 / FOLD)
+            tt(v("f2", 2 * a + 1, 2 * e, 2), (v("vv"), v("o_ft", a // 16, e // 16)), v("vv2", a, e), A.is_gt)
+            scan(v("o2", 2 * a, 2 * e), v("f2", 2 * a, 2 * e), v("d2", 2 * a, 2 * e), sgf, A.add, A.min)
+            ts(v("o_a", a // 16, e // 16), v("o2", 2 * a + 31, 2 * e, 32), sgf, A.subtract, FOLD, A.mult)
         if last:
-            act(v("ao"), v("o2", 2, 3 * C, 3))
+            act(v("ao"), (v("twice"), v("o_a")))
             store("Y", T.oa[:], v("ao"), slice(0, 128, 16))
         for h, (a, e) in enumerate(HALVES):
-            for b in (2, 3):
-                act(v("ph", C * b - NE + a, C * b - NE + e), (v("bw", CB * b, CB * b + CB), v("o_a", a // 16, e // 16)))
-                tt(v("yt", 4 * a + b, 4 * e, 4), v("ph", C * b - NE + a, C * b - NE + e), v("pb%d" % (b + 2), a, e), A.add)
-            for b in (0, 1):
-                tt(v("yt", 4 * a + b, 4 * e, 4), (v("bw", CB * b, CB * b + CB), v("o_a", a // 16, e // 16)),
-                   v("fh", C * b + a, C * b + e), A.add)
+            for b in ((0, 1, 2, 3), (0, 2, 3, 1))[h]:
+                pick = (v("bw", 2 * CB * b, 2 * CB * b + 2 * CB), v("o_a", a // 16, e // 16))
+                if b < 2:
+                    tt(v("yt", 4 * a + b, 4 * e, 4), pick, v("fh", C * b + a, C * b + e), A.add)
+                else:
+                    act(v("ph", C * b - NE + a, C * b - NE + e), pick)
+                    tt(v("yt", 4 * a + b, 4 * e, 4), v("ph", C * b - NE + a, C * b - NE + e), v("pb%d" % (b + 2), a, e), A.add)
             qz(v("yq", a, e), v("ys", a, e), v("yt", 4 * a, 4 * e))
         for h, (a, e) in enumerate(HALVES):
             for b, bank in enumerate((6, 7, 4, 5)):
@@ -462,7 +520,7 @@ def rank_program(g, core, T, topo):
             for b in range(4):
                 tt(v("xs", 4 * a + b, 4 * e, 4), v("rl", C * b + a, C * b + e), v("pb%d" % b, a, e), A.add)
             qz(v(nq, a, e), v(nsc, a, e), v("xs", 4 * a, 4 * e))
-            q, s, out = ("vq", "vs", "yo") if last else ("up", "ups", "sc1")
+            q, s, out = ("vq", "vs", "s2") if last else ("up", "ups", "sc1")
             mm(6 + h, q, s, 0, nq, nsc, a, e)
             if h == 0:
                 act(v(out, a, e), pb(6, e - a))
@@ -470,11 +528,9 @@ def rank_program(g, core, T, topo):
                 cp(v(out, a, e), pb(7, e - a))
             if last:
                 store("Y", T.oc[:, 4 * a:4 * e], v(nq, a, e), None, LOCAL + 1 - h)
-                store("SY"[h], T.y[:, a:e], v("yo", a, e), None, LOCAL + 1 - h)
+                store("SY"[h], T.y[:, a:e], v("s2", a, e), None, LOCAL + 1 - h)
+        turns.append((" ".join([ROUTES if t else ROUTES_FIRST, SOURCES, LAYER.replace("tq", nq)]), calls[mark:]))
+        mark = len(calls)
     for q in range(4):
         store("SY"[q % 2], T.osc[4 * q:4 * q + 4, :], v("ts%d" % R), slice(32 * q, 32 * q + 4), LOCAL - 0.5)
     issue_all()
-
-
-SLACK = 0.15
-PIECES = ((0, C), (C, NE))

from concourse.mybir import dt, AluOpType, ActivationFunctionType

C, L, S, R = 288, 48, 12, 3
NE = 2 * C
CB = C + L
HALVES = ((0, 160), (160, C))
BIG = 1e29
FOLD = 1024.0
MID = CB // 2
ROUND1, ROUND4 = 1.5 * 2.0 ** 23, 1.5 * 2.0 ** 25
CYCLE, GATHER, SCATTER, LIST_CALL, G_CALL, WAKE = 0.00083, 1.56, 3.5, 0.06, 0.15, 0.2
DMA_CALL, LOCAL, REMOTE_CALL, REMOTE, COLUMN, FIRST = 0.1, 1.5, 0.3, 2.2, 0.01, 2.5
SLACK = 0.15
ROUTES_FIRST = ("o_rt sa w64 w64 whi tq0 sb2 uq ss up ss o_z r64 o_ft zq zq zt zt zs zs dw se mb ab64 ab64 mb dw u64 mb lef "
                "v64 lef w64 lef o_d o_d lef yh eq yh eq de eq oe ptab eq zf zf o_p eq o_p se l1 l1 eq rr o_r l1 o_ft3 "
                "sa sa f01 o_s f01 mo df gw l0 l0 tp l2 tp o_l gw f3 vv d3 f3 f3")
ROUTES = "z z mb mb mb lef lef yh yh f01 de f01 oe f01 df vq l0 l0 l2 o_l d3 s2 gw tp tp gw f3 vv f3 f3"
SOURCES = "ab ab vv2 vv2 f2 f2 o2 o2 o_a o_a"
LAYER = "yt yt yt yt yt yq yt yt yt yq xs xs xs xs tq xs xs xs xs tq sc1"
F32, BF, I32, U16, H = "float32", "bfloat16", "int32", "uint16", "float16"
CODE, PLANE = "float8_e4m3fn_x4", "uint8"
A = AluOpType
AF = ActivationFunctionType

SCRATCH = {}


def _sb(names, n, d):
    for x in names.split():
        SCRATCH[x] = ("sbuf", [128, n], d)


_sb("xin xs yt dg", 4 * C, BF)
_sb("ut vt", 512, BF)
_sb("uq up vq", 128, CODE)
_sb("us ups vs", 128, PLANE)
_sb("wq", 512, CODE)
_sb("wp", 512, PLANE)
_sb("tq0 tq1 tq2 tq3 lq0 lq1 lq2 yq", C, CODE)
_sb("ts0 ts1 ts2 ts3 ls0 ls1 ls2 ys", C, PLANE)
_sb("diag dhalf", 516, BF)
_sb("eq", 768, CODE)
_sb("es", 768, PLANE)
_sb("mk mseg md lef ph wlo whi winv", NE, BF)
_sb("rti iw", 36, I32)
_sb("fti", 18, I32)
_sb("x64 x64b", 64, I32)
_sb("isw", 4, I32)
_sb("ik ikb", 2, I32)
_sb("o_rt o_z o_d o_p o_r o_s o_l", 36, U16)
_sb("o_ft o_ft3 o_a", 18, U16)
_sb("o_u", 8, U16)
_sb("o_sw", 4, U16)
_sb("oe le", 8 * R, U16)
_sb("m16", 16, F32)
_sb("col", 6, F32)
_sb("tw sa sb2 se rr", 36, F32)
_sb("l0 l1 l2", 72, F32)
_sb("ab64 u64 v64 w64 r64", 64, F32)
_sb("wt", 432, BF)
_sb("wi f01", C, BF)
_sb("ss rl", 4 * C, F32)
_sb("sc1 s2 m1 mo tp vv vv2 ao", C, F32)
_sb("fh", 2 * C, BF)
_sb("zq zt zs zf ptab tio z", NE, F32)
_sb("mb yf", NE + 16, F32)
_sb("wr", NE + 2, H)
_sb("dw yh", NE, H)
_sb("de", L, H)
_sb("ge", L, F32)
_sb("gw", 2 * L, F32)
_sb("f3 ab", 3 * C, BF)
_sb("d3", 3 * C, H)
_sb("f2", NE, BF)
_sb("d2 o2", NE, H)
_sb("own", C, BF)
_sb("twice", 2 * CB, F32)
_sb("df jg", C, H)
_sb("bw", 8 * CB, BF)
for _b in range(8):
    SCRATCH["pb%d" % _b] = ("psum", [128, 512], F32)

LOADS = ["x", "rt", "u", "ft", "wc", "ws", "v"]
SEMAPHORES = (["cV", "cS", "cP", "cG", "sent", "outY", "outS"] + ["ld_" + k for k in LOADS]
              + ["at%d" % t for t in range(R)] + ["ae%d" % t for t in range(R)])


def rank_program(g, core, T, topo):
    rank = T.rank_of(core)
    if rank is None:
        return
    N = len(T.cores)
    queue = {"V": g.vector, "S": g.scalar, "P": g.tensor, "G": g, "Y": g.sync}
    turns = []
    calls = []
    seen = {k: [] for k in SCRATCH}

    def v(name, a=0, b=None, s=1):
        return (name, a, SCRATCH[name][1][1] if b is None else b, s)

    def ap(x):
        if not isinstance(x, tuple):
            return x
        if len(x) == 2:
            w = ap(x[0])
            if SCRATCH[x[0][0]][2] == CODE:
                w = w.bitcast(dt.uint32)
            return w.indirect(ap(x[1]))
        return T[x[0]][:, x[1]:x[2]:x[3]] if x[3] > 1 else T[x[0]][:, x[1]:x[2]]

    def touched(outs, ins):
        r = []
        for xs, w in ((outs, True), (ins, False)):
            for x in xs:
                if isinstance(x, tuple):
                    r += [(x[0], w), (x[1], False)] if len(x) == 2 else [(x, w)]
        return [(x[0], {0} if SCRATCH[x[0]][0] == "psum" else set(range(x[1], x[2], x[3])), w) for x, w in r]

    def note(e, outs, ins, issue, busy, sem, adds, late=0.0, after=()):
        c = {"e": e, "issue": issue, "busy": busy, "sem": sem, "adds": adds, "late": late, "deps": set(after), "i": len(calls),
             "name": (outs[0] if len(outs[0]) == 4 else outs[0][0])[0] if outs else ""}
        acc = touched(outs, ins)
        for name, cols, w in acc:
            bank = SCRATCH[name][0] == "psum"
            c["deps"] |= {c2["i"] for cols2, w2, c2 in seen[name] if (w or w2 or (bank and c2["e"] != e)) and cols & cols2}
        for name, cols, w in acc:
            if w:
                seen[name] = [k for k in seen[name] if not k[0] <= cols]
        for name, cols, w in acc:
            seen[name].append([cols, w, c])
        calls.append(c)
        return c["i"]

    def width(x):
        return 16 * width(x[1]) if len(x) == 2 else len(range(x[1], x[2], x[3]))

    def op(e, outs, ins, call, cycles=1.0):
        views = [x for x in outs + ins if isinstance(x, tuple)]
        n = max(width(x) for x in outs)
        if len(outs[0]) == 2:
            busy = LIST_CALL + SCATTER * n * CYCLE
        elif any(len(x) == 2 for x in views):
            busy = LIST_CALL + GATHER * n * CYCLE
        else:
            short = e == "V" and cycles == 1.0 and all(SCRATCH[x[0]][2] in (BF, H, U16) for x in views if width(x) == n)
            busy = max(64, n * cycles * (0.5 if short else 1.0)) * CYCLE + (G_CALL if e == "G" else 0.0)
        note(e, outs, ins, lambda: call().then_inc(T.sem["c" + e], 1), busy, "c" + e, 1)

    def raw(x):
        return ap(x).bitcast(dt.uint8) if SCRATCH[x[0]][2] == CODE else ap(x)

    def load(e, name, out, late, after=()):
        return note(e, [out], [], lambda: queue[e].dma_start(raw(out), T[name][:]).then_inc(T.sem["ld_" + name], 16),
                    DMA_CALL, "ld_" + name, 16, late, after)

    def store(e, out, x, rows=None, late=LOCAL):
        src = raw(x) if rows is None else T[x[0]][rows, x[1]:x[2]]
        note(e, [], [x], lambda: queue[e].dma_start(out, src).then_inc(T.sem["out" + e], 16), DMA_CALL, "out" + e, 16, late)

    def send(t, pairs, sem, first=0.0, late=0.0):
        dst = T.cores[(rank + 1 + t) % N]
        rid, pid = topo.addr(dst, core)

        def issue():
            for out, a in pairs:
                g.remote_dma(raw(out), raw(a), T.sem[sem], T.sem.sent, pid, rid, topo.mask(core, dst))
        return note("G", [], [a for out, a in pairs], issue, first + REMOTE_CALL * len(pairs), "sent",
                    len(pairs) * len(topo.engines(core, dst)), late)

    def arrive(t, outs, sem, writes, late, after):
        note(None, outs, [], None, 0.0, sem, writes * len(topo.engines(T.cores[(rank - 1 - t) % N], core)), late, after)

    def issue_all():
        users, follows, before = [[] for c in calls], [[] for c in calls], None
        for c in calls:
            c["left"], c["ready"] = len(c["deps"]), 0.0
            for d in c["deps"]:
                users[d].append(c)
        for names, pool in turns:
            for name in names.split():
                c = next((k for k in pool if k["e"] == "V" and k["name"] == name), None)
                if c:
                    pool.remove(c)
                    if before:
                        follows[before["i"]].append(c)
                        c["left"] += 1
                    before = c
        first_list = next(c for c in calls if c["sem"] == "ae0")
        for c in calls:
            if c["e"] == "G" and c["name"] == "bw":
                follows[min(first_list["deps"])].append(c)
                c["left"] += 1
        left = [c["left"] for c in calls]
        ranked = [c for c in calls if not c["left"]]
        for c in ranked:
            for u in users[c["i"]] + follows[c["i"]]:
                left[u["i"]] -= 1
                if not left[u["i"]]:
                    ranked.append(u)
        for c in reversed(ranked):
            c["way"] = c["busy"] + max([c["late"]] + [c["late"] + WAKE + u["way"] for u in users[c["i"]]]
                                       + [u["way"] for u in follows[c["i"]]])
            if c["sem"][:3] == "ld_":
                c["way"] = 1e3 - c["i"]
        free = {e: 0.0 for e in list(queue) + [None]}
        open_, order = [c for c in calls if not c["left"]], []
        while open_:
            now = {e: max(free[e], min(c["ready"] for c in open_ if c["e"] == e)) for e in {c["e"] for c in open_}}
            e = min(now, key=lambda k: (now[k], str(k)))
            mine = [c for c in open_ if c["e"] == e]
            c = max((k for k in mine if k["ready"] <= now[e]), key=lambda k: (k["way"], -k["i"]))
            gain, first = SLACK, c
            for k in mine:
                at = max(now[e], k["ready"])
                ahead = max(now[e] + c["way"], max(at, now[e] + c["busy"]) + k["way"]) - max(at + k["way"], at + k["busy"] + c["way"])
                if ahead > gain:
                    gain, first = ahead, k
            c = first
            start = max(now[e], c["ready"])
            if e is not None:
                free[e] = start + c["busy"]
            open_.remove(c)
            order.append(c)
            for u in users[c["i"]]:
                u["ready"] = max(u["ready"], start + c["busy"] + c["late"] + (WAKE if u["e"] else 0.0))
            for u in users[c["i"]] + follows[c["i"]]:
                u["left"] -= 1
                if not u["left"]:
                    open_.append(u)
        count, known = {}, {e: {} for e in queue}
        for c in order:
            e = c["e"]
            count[c["sem"]] = count.get(c["sem"], 0) + c["adds"]
            c["count"], c["clock"] = count[c["sem"]], {}
            if e is None:
                continue
            best = {}
            for d in [calls[i] for i in c["deps"]]:
                if d["count"] > best.get(d["sem"], {"count": 0})["count"]:
                    best[d["sem"]] = d
            for s, d in best.items():
                if known[e].get(s, 0) < d["count"] and not any(k["clock"].get(s, 0) >= d["count"] for k in best.values()):
                    queue[e].wait_ge(T.sem[s], d["count"])
            for s, d in best.items():
                for s2, n2 in list(d["clock"].items()) + [(s, d["count"])]:
                    known[e][s2] = max(known[e].get(s2, 0), n2)
            c["clock"] = dict(known[e])
            c["issue"]()
        for s in ("cG", "sent", "cP", "cV", "cS"):
            g.wait_ge(T.sem[s], count[s])
        g.sync.wait_ge(T.sem.outY, count["outY"])
        g.scalar.wait_ge(T.sem.outS, count["outS"])

    V, Sc, P = g.vector, g.scalar, g.tensor

    def cp(out, a):
        o = ap(out).bitcast(dt.uint32) if len(out) == 4 and SCRATCH[out[0]][2] == CODE else ap(out)
        op("V", [out], [a], lambda: V.tensor_copy(o, ap(a)))

    def tt(out, a, b, o):
        op("V", [out], [a, b], lambda: V.tensor_tensor(ap(out), ap(a), ap(b), o),
           1.0 if "psum" in (SCRATCH[a[0]][0] if len(a) == 4 else "", SCRATCH[b[0]][0]) else 2.0)

    def ts(out, a, s1, o0, s2=None, o1=None):
        if o1 is None:
            op("V", [out], [a, s1], lambda: V.tensor_scalar(ap(out), ap(a), ap(s1), None, o0))
        else:
            op("V", [out], [a, s1, s2], lambda: V.tensor_scalar(ap(out), ap(a), ap(s1), ap(s2), o0, o1))

    def scan(out, d0, d1, ini, o0, o1):
        op("V", [out], [d0, d1, ini], lambda: V.tensor_tensor_scan(ap(out), ap(d0), ap(d1), ap(ini), o0, o1))

    def ms(out, c):
        op("V", [out], [], lambda: V.memset(ap(out), c))

    def turn(out, a):
        op("V", [out], [a], lambda: V.transpose(ap(out), ap(a)))

    def qz(q, s, a):
        op("V", [q, s], [a], lambda: V.quantize_mx(ap(q), ap(s), ap(a)), 1.1)

    def act(out, a, f=AF.Identity, bias=0.0, scale=1.0):
        if f is AF.Copy:
            op("S", [out], [a], lambda: Sc.activation(ap(out), ap(a), f))
        else:
            op("S", [out], [a, bias, scale], lambda: Sc.activation(ap(out), ap(a), f, bias=ap(bias), scale=ap(scale)))

    def fill(out, c):
        act(out, v("mseg", 0, width(out)), bias=c, scale=0.0)

    def pb(bank, n):
        return v("pb%d" % bank, 0, n)

    def mm(bank, lq, ls, i, rq, rs, a=0, b=C):
        x = [v(lq, 128 * i, 128 * i + 128), v(ls, 128 * i, 128 * i + 128), v(rq, a, b), v(rs, a, b)]
        op("P", [pb(bank, b - a)], x, lambda: P.matmul_mx(ap(pb(bank, b - a)), ap(x[0]), ap(x[1]), ap(x[2]), ap(x[3]), True, True), 0.8)

    def copy(out, a):
        op("G", [out], [a], lambda: g.affine_select(ap(out), ap(a), [[0, width(out)]], A.is_ge, 0.0, 0, 0), 2.0)

    def iota(out, pat, base, cm):
        if SCRATCH[out[0]][2] == I32:
            op("G", [out], [], lambda: g.iota(ap(out), pat, base, cm), 2.0)
        else:
            op("G", [out], [], lambda: g.iota(ap(out), pat, base, cm, allow_small_or_imprecise_dtypes=True), 2.0)

    sg, sgr, k16, sgf = [v("col", i, i + 1) for i in range(4)]

    def fold(out, a, n, m=0):
        scan(v(out, m, n), v("md", m, n), a, sg, A.add, A.min)
        return v(out, 15, n, 16)

    load("S", "rt", v("rti"), LOCAL)
    load("S", "u", v("ut"), LOCAL + 1.3)
    for name, buf, late in (("x", "xin", 1.0), ("ft", "fti", 1.5), ("v", "vt", 25.0), ("wc", "wq", 3.0), ("ws", "wp", 3.0)):
        load("Y", name, v(buf), LOCAL + late)

    iota(v("x64"), [[0, 4], [1, 16]], 128, -1)
    iota(v("ik"), [[0, 2]], 0, 1)
    iota(v("iw"), [[16, 36]], 0, 0)
    iota(v("isw"), [[16, 2], [32, 2]], 0, 0)
    iota(v("tio"), [[1, NE]], 0, 0)
    ts(v("x64b"), v("x64"), 15, A.bitwise_and)
    ts(v("m16"), v("x64b", 0, 16), 0.0, A.is_equal)
    ts(v("u64"), v("x64b"), 0.0, A.is_equal, 2 * FOLD, A.mult)
    ts(v("v64"), v("x64b"), 1.0, A.is_equal, -FOLD, A.mult)
    tt(v("md", 0, 64), v("u64"), v("v64"), A.add)
    for n in range(64, NE, 64):
        act(v("md", n, n + 64), v("md", 0, 64))
    ts(sg, v("m16", 15, 16), FOLD, A.mult, -FOLD, A.add)
    ts(sgr, v("m16", 15, 16), FOLD, A.mult, 0.5 * (S - 1) - FOLD, A.add)
    ts(v("ikb"), v("ik"), 15, A.bitwise_and)
    cp(k16, v("ikb", 0, 1))
    cp(v("o_u"), v("iw", 0, 8))
    ts(v("tw"), v("iw"), k16, A.add)
    ts(v("o_sw"), v("isw"), k16, A.add)
    ms(v("mseg"), 1.0)
    ms(v("mseg", 0, NE, 16), 0.0)
    fill(v("mk"), BIG)
    fill(v("mk", S - 1, NE, S), -BIG)
    ms(v("mb", 0, C + 1, 96), -BIG)
    ms(v("yf", 0, 1), 0.0)
    ms(v("wr", NE, NE + 2), 512.0)
    ms(v("oe"), 0)
    ms(v("ab64"), 0.0)
    ms(v("w64"), 0.0)
    fill(v("f3", 0, 3 * C, 3), 0.0)
    act(v("f2", 0, NE, 2), v("md", 0, C), scale=1 / FOLD)
    act(v("own"), v("md", 0, C), AF.Relu)
    act(v("own"), v("own"), bias=BIG, scale=-BIG / FOLD)
    for w in (0, CB):
        act(v("twice", w, w + CB), v("tio", 0, CB))
    ts(sgf, v("m16", 15, 16), -1.0, A.add)
    fill(v("l0", 0, 72, 2), 0.0)
    fill(v("l1", 36, 72, 2), float(L))
    ms(v("wt", 0, 144), 0.0)
    ms(v("wt", C, 432), 0.0)
    for c in range(9):
        act(v("wt", 144 + 16 * c, 160 + 16 * c), v("m16"), scale=4.0 ** c)
        act(v("wi", 16 * c, 16 * c + 16), v("m16"), scale=0.25 ** c)
    act(v("wi", 144, C), v("wi", 0, 144))
    op("G", [v("diag")], [v("mseg")],
       lambda: g.affine_select(T.diag[:], T.mseg[:, 0:516], [[-1, 516]], A.is_equal, 0.0, 3, 4), 2.0)
    act(v("dhalf"), v("diag"), scale=0.5)
    mark = len(calls)
    for i, (src, b) in enumerate([("diag", b) for b in range(4)] + [("dhalf", 2), ("dhalf", 3)]):
        qz(v("eq", 128 * i, 128 * i + 128), v("es", 128 * i, 128 * i + 128), v(src, 3 - b, 515 - b))

    qz(v("tq0"), v("ts0"), v("xin"))
    qz(v("uq"), v("us"), v("ut"))
    cp(v("up"), (v("uq"), v("o_u")))
    act(v("ups"), (v("us"), v("o_u")), AF.Copy)
    mm(4, "up", "ups", 0, "tq0", "ts0", 0, 144)
    mm(5, "up", "ups", 0, "tq0", "ts0", 144, C)
    act(v("sc1", 0, 144), pb(4, 144))
    act(v("sc1", 144, C), pb(5, 144))

    cp(v("o_rt"), v("rti"))
    cp(v("o_ft"), v("fti"))
    ts(v("o_ft3"), v("fti"), 3.0, A.mult, 2.0, A.add)
    act(v("wr", 0, NE), (v("tio", 0, C), v("o_rt")), bias=512.0)
    scan(v("dw"), v("wr", 0, NE), v("wr", 1, NE + 1), 0.0, A.max, A.subtract)
    ts(v("dw", S - 1, NE, S), v("wr", S - 1, NE, S), -512.0, A.add)
    act(v("wlo"), (v("wt", 144, 432), v("o_rt")))
    cp(v("whi"), (v("wt", 0, C), v("o_rt")))
    act(v("winv"), (v("wi"), v("o_rt")))
    ts(v("sa"), v("rti"), 144.0, A.is_ge, float(NE), A.mult)
    tt(v("sb2"), v("sa"), v("tw"), A.add)
    cp(v("o_z"), v("sb2"))
    scan(v("ss", 0, NE), v("wlo"), v("wlo"), 0.5, A.add, A.max)
    scan(v("ss", NE, 2 * NE), v("whi"), v("whi"), 0.5, A.add, A.max)
    for a, e in ((0, 320), (320, NE)):
        tt(v("zq", a, e), (v("ss"), v("o_z", a // 16, e // 16)), v("winv", a, e), A.mult)
        turn(v("zt", a, e), v("zq", a, e))
        scan(v("zs", a, e), v("mseg", a, e), v("zt", a, e), 0.0, A.mult, A.add)
    ts(v("w64", 0, 18), v("rti", 0, 36, 2), 2.0, A.mult)
    ts(v("w64", 32, 50), v("rti", 1, 36, 2), 2.0, A.mult)
    turn(v("r64"), v("w64"))
    ts(v("se"), v("zs", 15, NE, 16), ROUND4, A.add, ROUND4, A.subtract)
    tt(v("ab64", 0, 18), v("se", 0, 36, 2), v("zs", 15, NE, 32), A.is_gt)
    tt(v("ab64", 32, 50), v("se", 1, 36, 2), v("zs", 31, NE, 32), A.is_gt)
    turn(v("u64"), v("ab64"))
    tt(v("v64"), (v("u64"), v("o_sw")), v("r64"), A.add)
    turn(v("w64"), v("v64"))
    cp(v("o_d", 0, 36, 2), v("w64", 0, 18))
    cp(v("o_d", 1, 36, 2), v("w64", 32, 50))
    cp((v("ptab"), v("o_d")), v("tio"))
    for a, e in ((C, NE), (0, C)):
        fold("zf", v("ptab", a // C, NE, 2), e, a)
        ts(v("o_p", a // 16, e // 16), v("zf", a + 15, e, 16), sg, A.subtract)
    pw = v("zf", 15, NE, 16)
    ts(v("se"), pw, sgr, A.subtract, 1.0 / S, A.mult)
    ts(v("rr"), v("se"), ROUND1, A.add, ROUND1, A.subtract)
    ts(v("o_r"), v("se"), ROUND1, A.add, ROUND1, A.subtract)
    tt(v("l1", 0, 36, 2), v("zf", 15, C, 16), v("zf", C + 15, NE, 16), A.subtract)
    ts(v("l1", 1, 36, 2), v("zf", C + 15, NE, 16), sg, A.subtract)
    ts(v("l1", 37, 72, 2), v("se", 18, 36), ROUND1, A.add, ROUND1, A.subtract)
    tt(v("sa", 0, 18), v("tw", 0, 18), v("rr", 18, 36), A.subtract)
    tt(v("sa", 18, 36), v("rr", 18, 36), v("rr", 0, 18), A.subtract)
    ts(v("o_s"), v("sa"), float(L), A.add)
    act(v("jg"), (v("tio"), v("o_s", 0, 18)), bias=-float(CB))
    act(v("d3", 1, 3 * C, 3), (v("tio"), v("o_s", 18, 36)), bias=-float(L))
    act(v("d3", 2, 3 * C, 3), (v("tio"), v("o_r", 0, 18)), bias=float(C - MID))

    for t in range(R):
        tq, tsc, lq, lsc = "tq%d" % t, "ts%d" % t, "lq%d" % t, "ls%d" % t
        nq, nsc = "tq%d" % (t + 1), "ts%d" % (t + 1)
        le = v("le", 8 * t, 8 * t + 3)
        last = t == R - 1
        runs = ((0, C),) if t == 0 else HALVES
        sent = [send(t, [(v(lq, a, e), v(tq, a, e))], "at%d" % t, FIRST if t == 0 else 0.0, (C - a) * COLUMN) for a, e in runs]
        sent.append(send(t, [(v(lsc), v(tsc))], "at%d" % t))
        arrive(t, [v(lq), v(lsc)], "at%d" % t, len(sent), REMOTE + C * COLUMN / 4, sent)
        for b in range(4):
            mm(b, "eq", "es", b, tq, tsc)
            for w in (2 * b, 2 * b + 1):
                if t or w % 2 == 0:
                    act(v("bw", CB * w, CB * w + C), pb(b, C), scale=0.5)
                else:
                    copy(v("bw", CB * w, CB * w + C), v("bw", CB * w - CB, CB * w - L))
        for b in (0, 1):
            act(v("fh", C * b, C * b + C), pb(b, C), scale=0.5)
        for a, e in ((0, 192), (192, C)):
            (cp if t else act)(v("z", a, e), (v("sc1"), v("o_rt", a // 16, e // 16)))
        act(v("z", C, NE), (v("sc1"), v("o_rt", 18, 36)))
        for a, e in ((0, 192), (192, C), (C, NE)) if t else ((C, NE), (0, 192), (192, C)):
            scan(v("mb", a + 1, e), v("z", a, e - 1), v("mk", a, e - 1), -BIG, A.max, A.min)
        for a, e in ((0, C), (C, NE)) if t else ((416, NE), (C, 416), (0, 128), (128, C)):
            tt(v("lef", a, e), (v("sc1"), v("o_rt", a // 16, e // 16)), v("mb", a, e), A.is_le)
        for a, e in ((0, C), (C, NE)) if t else ((C, NE), (0, C)):
            scan(v("yh", a, e), v("lef", a, e), v("dw", a, e), 0.0, A.mult, A.add)
            act(v("yf", a + 1, e + 1), v("yh", a, e))
        ts(v("oe", 8 * t, 8 * t + 3), fold("de", v("yh", S - 1, NE, S), L), sg, A.subtract)
        arrive(t, [v("le", 8 * t, 8 * t + 4)], "ae%d" % t, 1, REMOTE,
               [send(t, [(v("le", 8 * t, 8 * t + 4), v("oe", 8 * t, 8 * t + 4))], "ae%d" % t)])
        act(v("m1"), (v("mb", 0, NE), v("o_p", 18, 36)))
        for a, e in ((0, 96), (96, 192), (192, C)) if t else HALVES:
            tt(v("f01", a, e), (v("mb", 0, NE), v("o_p", a // 16, e // 16)), v("m1", a, e), A.is_ge)
        fw = fold("df", v("f01"), C)
        ts(v("l0", 1, 36, 2), fw, sg, A.subtract)
        ts(v("l0", 37, 72, 2), fw, sg, A.subtract)
        scan(v("l2"), v("l0"), v("l1"), 0.0, A.mult, A.add)
        cp(v("o_l"), v("l2", 1, 72, 2))
        if t:
            act(v("mo"), (v("mb", 0, NE), v("o_l", 0, 18)))
        else:
            tt(v("mo"), (v("mb", 0, NE), v("o_p", 0, 18)), v("m1"), A.max)
        tt(v("d3", 0, 3 * C, 3), (v("yf", 0, NE), v("o_l", 0, 18)), v("jg"), A.add)
        if t == 1:
            qz(v("vq"), v("vs"), v("vt"))
        mm(6, "up", "ups", 0, lq, lsc, 0, 144)
        mm(7, "up", "ups", 0, lq, lsc, 144, C)
        (cp if t else act)(v("s2", 0, 144), pb(6, 144))
        act(v("s2", 144, C), pb(7, 144))
        for b, bank in enumerate((4, 5, 6, 7)):
            mm(bank, "eq", "es", b, lq, lsc)
            act(v("dg", C * b, C * b + C), pb(bank, C))
        for b in (2, 3):
            mm(b + 2, "eq", "es", b + 2, tq, tsc)
        gs, r0 = v("gw", 0, L), v("o_r", 0, 18)
        cp(gs, (v("s2"), le))
        act(v("ge"), gs, AF.Abs, 2.0 ** -125, 1.25 * 2.0 ** -24)
        tt(v("gw", L, 2 * L), gs, v("ge"), A.subtract)
        for w in range(8):
            act(v("bw", CB * w + C, CB * w + CB), (v("dg", C * (w // 2), C * (w // 2) + C), le), scale=0.5)
        for a, e in HALVES:
            tt(v("tp", a, e), (gs, v("o_r", 18 + a // 16, 18 + e // 16)), v("mo", a, e), A.max)
        tt(v("vv"), (gs, r0), v("tp"), A.max)
        for a, e in HALVES:
            scan(v("vv2", a, e), v("vv", a, e), v("own", a, e), BIG, A.min, A.max)
        for a, e in HALVES:
            tt(v("f3", 3 * a + 2, 3 * e, 3), (gs, v("o_r", a // 16, e // 16)), v("tp", a, e), A.is_lt)
            if a == 0:
                tt(v("f3", 1, 3 * C, 3), (v("gw"), v("o_l", 18, 36)), v("mo"), A.is_lt)
        for a, e in HALVES:
            scan(v("ab", 3 * a, 3 * e), v("f3", 3 * a, 3 * e), v("d3", 3 * a, 3 * e), 0.0, A.mult, A.add)
        for a, e in HALVES:
            act(v("d2", 2 * a, 2 * e, 2), v("ab", 3 * a + 2, 3 * e, 3), bias=MID / FOLD, scale=1 / FOLD)
            act(v("d2", 2 * a + 1, 2 * e, 2), (v("ab"), v("o_ft3", a // 16, e // 16)), bias=(CB + MID) / FOLD, scale=1 / FOLD)
            tt(v("f2", 2 * a + 1, 2 * e, 2), (v("vv"), v("o_ft", a // 16, e // 16)), v("vv2", a, e), A.is_gt)
            scan(v("o2", 2 * a, 2 * e), v("f2", 2 * a, 2 * e), v("d2", 2 * a, 2 * e), sgf, A.add, A.min)
            ts(v("o_a", a // 16, e // 16), v("o2", 2 * a + 31, 2 * e, 32), sgf, A.subtract, FOLD, A.mult)
        if last:
            act(v("ao"), (v("twice"), v("o_a")))
            store("Y", T.oa[:], v("ao"), slice(0, 128, 16))
        for h, (a, e) in enumerate(HALVES):
            for b in ((0, 1, 2, 3), (0, 2, 3, 1))[h]:
                pick = (v("bw", 2 * CB * b, 2 * CB * b + 2 * CB), v("o_a", a // 16, e // 16))
                if b < 2:
                    tt(v("yt", 4 * a + b, 4 * e, 4), pick, v("fh", C * b + a, C * b + e), A.add)
                else:
                    act(v("ph", C * b - NE + a, C * b - NE + e), pick)
                    tt(v("yt", 4 * a + b, 4 * e, 4), v("ph", C * b - NE + a, C * b - NE + e), v("pb%d" % (b + 2), a, e), A.add)
            qz(v("yq", a, e), v("ys", a, e), v("yt", 4 * a, 4 * e))
        for h, (a, e) in enumerate(HALVES):
            for b, bank in enumerate((6, 7, 4, 5)):
                mm(bank, "wq", "wp", b, "yq", "ys", a, e)
                act(v("rl", C * b + a, C * b + e), pb(bank, e - a), AF.Relu, 0.0, 0.03125)
        for h, (a, e) in enumerate(HALVES):
            for b in range(4):
                tt(v("xs", 4 * a + b, 4 * e, 4), v("rl", C * b + a, C * b + e), v("pb%d" % b, a, e), A.add)
            qz(v(nq, a, e), v(nsc, a, e), v("xs", 4 * a, 4 * e))
            q, s, out = ("vq", "vs", "s2") if last else ("up", "ups", "sc1")
            mm(6 + h, q, s, 0, nq, nsc, a, e)
            if h == 0:
                act(v(out, a, e), pb(6, e - a))
            else:
                cp(v(out, a, e), pb(7, e - a))
            if last:
                store("Y", T.oc[:, 4 * a:4 * e], v(nq, a, e), None, LOCAL + 1 - h)
                store("SY"[h], T.y[:, a:e], v("s2", a, e), None, LOCAL + 1 - h)
        turns.append((" ".join([ROUTES if t else ROUTES_FIRST, SOURCES, LAYER.replace("tq", nq)]), calls[mark:]))
        mark = len(calls)
    for q in range(4):
        store("SY"[q % 2], T.osc[4 * q:4 * q + 4, :], v("ts%d" % R), slice(32 * q, 32 * q + 4), LOCAL - 0.5)
    issue_all()
